import numpy as np
import ml_dtypes


def mxq(x, axis, fmt="e4m3"):
    dtype, down = {"e4m3": (ml_dtypes.float8_e4m3fn, 7), "e5m2": (ml_dtypes.float8_e5m2, 14)}[fmt]
    v = np.moveaxis(np.asarray(x, np.float32).astype(ml_dtypes.bfloat16).astype(np.float64), axis, -1)
    blocks = v.reshape(v.shape[:-1] + (-1, 32))
    amax = np.abs(blocks).max(-1, keepdims=True)
    byte = np.maximum(np.where(amax > 0, np.frexp(amax)[1] - 1 + 127, 0) - down, 1)
    scale = np.exp2(byte - 127.0)
    codes = (blocks / scale).astype(np.float32).astype(dtype).astype(np.float64)
    return np.moveaxis((codes * scale).reshape(v.shape), -1, axis)


WIDE = False


def mx_kscale(k):
    if not WIDE:
        return np.ones(k)
    levels = np.array([10, -10, 5, -5, 0])
    if k % 512:
        return np.exp2(np.random.permutation(np.resize(levels, k // 32))).repeat(32)
    a = np.empty((k // 512, 16))
    for p in range(k // 512):
        a[p, :8] = np.random.permutation(np.resize(levels, 8))
        for g in range(8):
            far = levels[np.abs(levels - a[p, g]) >= 10]
            a[p, g + 8] = far[np.random.randint(len(far))]
    return np.exp2(a.ravel()).repeat(32)


def f64(x):
    return np.asarray(x).astype(np.float64)


def striped(idx):
    return np.tile(idx.reshape(-1, 16).T, (8, 1)).astype(np.uint16)


def unstriped(offs):
    return offs[:16].T.reshape(-1).astype(np.int64)


def relu(v):
    return np.maximum(v, 0.0)


K, T, D, S, V, H, N = 1024, 2048, 3, 512, 256, 512, 128
P = 2 ** 7


def setup_inputs():
    n = np.random.standard_normal
    s = mx_kscale(K)[:, None]
    u = mx_kscale(H)
    q = np.random.permutation(S)
    return {
        "xT": (n((K, T)) * s).astype(np.float32),
        "w1": (n((K, H)) / np.sqrt(K) / s * u).astype(np.float32),
        "w2": (n((H, N)) / np.sqrt(H) / u[:, None]).astype(np.float32),
        "gate": np.tile(np.random.uniform(0.2, 1.0, (D, 1, V)) / np.sqrt(D), (1, P, 1)).astype(np.float32),
        "offs": striped(np.random.permutation(T)[:S]),
        "pos1": striped(q[:V]),
        "pos2": striped(q[V:]),
        "pos3": striped(np.random.permutation(S)[:V]),
    }


def reference(xT, w1, w2, gate, offs, pos1, pos2, pos3):
    h = relu(mxq(f64(w1), 0, "e4m3").T @ mxq(f64(xT)[:, unstriped(offs)], 0, "e4m3"))
    z = sum(f64(gate)[d, :1] * h[:, unstriped(p)] for d, p in enumerate((pos1, pos2, pos3)))
    return mxq(f64(w2), 0, "e4m3").T @ mxq(z, 0, "e4m3")

@@ -1,0 +1,187 @@
+from contextlib import ExitStack
+
+import concourse.mybir as mybir
+
+K, T, D, S, V, H, N = 1024, 2048, 3, 512, 256, 512, 128
+P = 128
+PACK = 4
+PASSES = K // (P * PACK)
+FLOPS = 2 * K * S * H + 2 * H * V * N
+
+F32 = mybir.dt.float32
+BF16 = mybir.dt.bfloat16
+U32 = mybir.dt.uint32
+U16 = mybir.dt.uint16
+U8 = mybir.dt.uint8
+FP8X4 = mybir.dt.float8_e4m3fn_x4
+ADD = mybir.AluOpType.add
+MULT = mybir.AluOpType.mult
+RELU = mybir.ActivationFunctionType.Relu
+
+
+def tile_picked_sage_relu_e_kernel(tc, xT, w1, w2, gate, offs, pos1, pos2, pos3, out):
+    nc = tc.nc
+    with ExitStack() as ctx:
+        keep = ctx.enter_context(tc.tile_pool(name="keep", bufs=1))
+        psum = ctx.enter_context(tc.psum_pool(name="psum", bufs=1))
+
+        offs_t = keep.tile([P, S // 16], U16, name="offs_t")
+        pos_t = [keep.tile([P, V // 16], U16, name=f"pos_t{d}") for d in range(D)]
+        nc.sync.dma_start(offs_t[:], offs)
+
+        x_rows = xT.rearrange("(s p j) t -> s p j t", p=P, j=PACK)
+        w1_rows = w1.rearrange("(s p j) c -> s p j c", p=P, j=PACK)
+        pieces = [[(0, 2), (2, 2)], [(0, 1), (1, 1), (2, 1), (3, 1)]]
+        w1_raw0 = keep.tile([P, PACK, H], F32, name="w1_raw0")
+        pairs = [keep.tile([P, 2, H], F32, name=f"w1_raw1_{b}") for b in range(2)]
+        w2_raw = keep.tile([P, PACK, N], F32, name="w2_raw")
+        gates = keep.tile([P, D, V], F32, name="gates")
+        plane = {}
+
+        nc.sync.dma_start(w1_raw0[:], w1_rows[0])
+        for s in range(PASSES):
+            for j0, n in pieces[s]:
+                x_t = keep.tile([P, n, T], F32, name=f"x{s}_{j0}")
+                nc.sync.dma_start(x_t[:], x_rows[s][:, j0 : j0 + n, :])
+                for j in range(n):
+                    plane[s, j0 + j] = x_t[:, j, :]
+        for b in range(2):
+            nc.sync.dma_start(pairs[b][:], w1_rows[1][:, 2 * b : 2 * b + 2, :])
+        nc.sync.dma_start(gates[:], gate.rearrange("d p v -> p d v"))
+        for d, p in enumerate((pos1, pos2, pos3)):
+            nc.sync.dma_start(pos_t[d][:], p)
+        w2_rows = w2.rearrange("(g t r) m -> t g r m", t=PACK, r=8)
+        for t in range(PACK):
+            nc.sync.dma_start(w2_raw[:, t, :], w2_rows[t])
+
+        xg = [keep.tile([P, S, PACK], BF16, name=f"xg{s}", align_bytes=64) for s in range(PASSES)]
+        x_codes = [keep.tile([P, S], U32, name=f"x_codes{s}", align_bytes=64) for s in range(PASSES)]
+        x_scales = [keep.tile([P, S], U8, name=f"x_scales{s}", align_bytes=64) for s in range(PASSES)]
+        w1g = [keep.tile([P, H * PACK], BF16, name=f"w1g{s}", align_bytes=64) for s in range(PASSES)]
+        w1_codes = [keep.tile([P, H], U32, name=f"w1_codes{s}", align_bytes=64) for s in range(PASSES)]
+        w1_scales = [keep.tile([P, H], U8, name=f"w1_scales{s}", align_bytes=64) for s in range(PASSES)]
+
+        def quantize(codes, scales, grouped):
+            nc.vector.quantize_mx(out=codes.bitcast(FP8X4), scales=scales, in_=grouped)
+
+        def quantize_x(s):
+            quantize(x_codes[s][:], x_scales[s][:], xg[s][:].rearrange("p n j -> p (n j)"))
+
+        picked = [
+            keep.tile([P, PACK, S], F32, name="picked0", align_bytes=64),
+            keep.tile([P, 2, S], F32, name="picked1", align_bytes=64),
+        ]
+
+        def interleave(dst, src):
+            return dst.rearrange("p (c i) j -> p c j i", i=4), src.rearrange("p j (c i) -> p c j i", i=4)
+
+        def lay(engine_copy, raw, s, j0, j1, t0, t1):
+            engine_copy(
+                w1g[s][:].rearrange("p (t g r j) -> p t g r j", t=PACK, r=8, j=PACK)[:, t0:t1, :, :, j0:j1],
+                raw.rearrange("p j (g t r) -> p t g r j", t=PACK, r=8)[:, t0:t1],
+            )
+
+        lay(nc.scalar.copy, w1_raw0[:], 0, 0, PACK, 0, PACK)
+        for j in range(PACK):
+            nc.vector.tensor_copy(picked[0][:, j, :], plane[0, j].indirect(offs_t[:]))
+            if j == 1:
+                quantize(w1_codes[0][:], w1_scales[0][:], w1g[0][:])
+        nc.scalar.copy(*interleave(xg[0][:], picked[0][:]))
+        nc.vector.tensor_copy(picked[1][:, 0, :], plane[1, 0].indirect(offs_t[:]))
+        quantize_x(0)
+        nc.vector.tensor_copy(picked[1][:, 1, :], plane[1, 1].indirect(offs_t[:]))
+        nc.scalar.copy(*interleave(xg[1][:, :, 0:2], picked[1][:]))
+        nc.vector.tensor_copy(xg[1][:, :, 2], plane[1, 2].indirect(offs_t[:]))
+        nc.vector.tensor_copy(xg[1][:, :, 3], plane[1, 3].indirect(offs_t[:]))
+        quantize_x(1)
+        lay(nc.scalar.copy, pairs[0][:], 1, 0, 2, 0, 1)
+        lay(nc.scalar.copy, pairs[0][:], 1, 0, 2, 1, PACK)
+        for t in range(PACK):
+            lay(nc.scalar.copy if t >= 2 else nc.vector.tensor_copy, pairs[1][:], 1, 2, 4, t, t + 1)
+            if t != 1 and t != 2:
+                continue
+            cols = slice((t - 1) * P, t * P)
+            quantize(w1_codes[1][:, cols], w1_scales[1][:, cols], w1g[1][:, (t - 1) * P * PACK : t * P * PACK])
+        for t in (2, 3):
+            cols = slice(t * P, (t + 1) * P)
+            quantize(w1_codes[1][:, cols], w1_scales[1][:, cols], w1g[1][:, t * P * PACK : (t + 1) * P * PACK])
+
+        h = [keep.tile([P, S], F32, name=f"h{t}") for t in range(PACK)]
+        banks = []
+        for t in range(PACK):
+            w = S // 2 if t == 0 else S
+            banks.append([(c, w, psum.tile([P, w], F32, name=f"h_acc{t}_{c}")) for c in range(0, S, w)])
+        for s in range(PASSES):
+            for t in range(PACK):
+                for c, w, acc in banks[t]:
+                    nc.tensor.matmul_mx(
+                        out=acc[:],
+                        lhsT=w1_codes[s][:, t * P : (t + 1) * P].bitcast(FP8X4),
+                        lhsT_scale=w1_scales[s][:, t * P : (t + 1) * P],
+                        rhs=x_codes[s][:, c : c + w].bitcast(FP8X4),
+                        rhs_scale=x_scales[s][:, c : c + w],
+                        start=(s == 0),
+                        stop=(s == PASSES - 1),
+                    )
+        for t in range(PACK):
+            for c, w, acc in banks[t]:
+                if c == 0:
+                    nc.scalar.activation(h[t][:, c : c + w], acc[:], RELU)
+                else:
+                    nc.vector.tensor_scalar_max(h[t][:, c : c + w], acc[:], 0.0)
+
+        u = [keep.tile([P, PACK, V], F32, name=f"u{d}") for d in range(D)]
+        s01 = keep.tile([P, PACK, V], F32, name="s01")
+        w2g = keep.tile([P, N, PACK], BF16, name="w2g", align_bytes=64)
+        w2_codes = keep.tile([P, N], U32, name="w2_codes", align_bytes=64)
+        w2_scales = keep.tile([P, N], U8, name="w2_scales", align_bytes=64)
+        nc.scalar.copy(*interleave(w2g[:], w2_raw[:]))
+        vh = V // 2
+
+        def fetch(t, d, v0, v1):
+            nc.vector.tensor_tensor(u[d][:, t, v0:v1], h[t][:].indirect(pos_t[d][:, v0 // 16 : v1 // 16]), gates[:, d, v0:v1], MULT)
+
+        def add_pair(t):
+            pair = slice(t, t + 2)
+            nc.vector.tensor_tensor(s01[:, pair, :], u[0][:, pair, :], u[1][:, pair, :], ADD)
+
+        for t in range(PACK - 1):
+            for d in range(D):
+                fetch(t, d, 0, V)
+            if t == 1:
+                add_pair(0)
+                quantize(w2_codes[:], w2_scales[:], w2g[:].rearrange("p m j -> p (m j)"))
+        fetch(PACK - 1, 0, 0, V)
+        fetch(PACK - 1, 1, 0, V)
+        fetch(PACK - 1, 2, 0, vh)
+        add_pair(2)
+        fetch(PACK - 1, 2, vh, V)
+
+        zg = keep.tile([P, V, PACK], BF16, name="zg", align_bytes=64)
+        z_codes = keep.tile([P, V], U32, name="z_codes", align_bytes=64)
+        z_scales = keep.tile([P, V], U8, name="z_scales", align_bytes=64)
+        for c in (0, vh):
+            nc.vector.tensor_tensor(
+                *interleave(zg[:, c : c + vh, :], s01[:, :, c : c + vh]),
+                u[2][:, :, c : c + vh].rearrange("p t (c i) -> p c t i", i=4),
+                ADD,
+            )
+        for c in (0, vh):
+            quantize(z_codes[:, c : c + vh], z_scales[:, c : c + vh], zg[:, c : c + vh, :].rearrange("p v j -> p (v j)"))
+        for c in (0, vh):
+            acc = psum.tile([P, vh], F32, name=f"o_acc{c}")
+            nc.tensor.matmul_mx(
+                out=acc[:],
+                lhsT=w2_codes[:].bitcast(FP8X4),
+                lhsT_scale=w2_scales[:],
+                rhs=z_codes[:, c : c + vh].bitcast(FP8X4),
+                rhs_scale=z_scales[:, c : c + vh],
+                start=True,
+                stop=True,
+            )
+            res = keep.tile([P, vh], F32, name=f"res{c}")
+            if c == 0:
+                nc.scalar.copy(res[:], acc[:])
+            else:
+                nc.vector.tensor_copy(res[:], acc[:])
+            nc.sync.dma_start(out[:, c : c + vh], res[:])

@@ -1,11 +1,13 @@
 from contextlib import ExitStack
 
 import concourse.mybir as mybir
+from concourse.masks import make_identity
 
 K, T, D, S, V, H, N = 1024, 2048, 3, 512, 256, 512, 128
 P = 128
 PACK = 4
 PASSES = K // (P * PACK)
+TILES = H // P
 FLOPS = 2 * K * S * H + 2 * H * V * N
 
 F32 = mybir.dt.float32
@@ -14,7 +16,6 @@ U32 = mybir.dt.uint32
 U16 = mybir.dt.uint16
 U8 = mybir.dt.uint8
 FP8X4 = mybir.dt.float8_e4m3fn_x4
-ADD = mybir.AluOpType.add
 MULT = mybir.AluOpType.mult
 RELU = mybir.ActivationFunctionType.Relu
 
@@ -32,156 +33,188 @@ def tile_picked_sage_relu_e_kernel(tc, xT, w1, w2, gate, offs, pos1, pos2, pos3,
         x_rows = xT.rearrange("(s p j) t -> s p j t", p=P, j=PACK)
         w1_rows = w1.rearrange("(s p j) c -> s p j c", p=P, j=PACK)
         pieces = [[(0, 2), (2, 2)], [(0, 1), (1, 1), (2, 1), (3, 1)]]
-        w1_raw0 = keep.tile([P, PACK, H], F32, name="w1_raw0")
-        pairs = [keep.tile([P, 2, H], F32, name=f"w1_raw1_{b}") for b in range(2)]
+        w1_raw = {(t, s): keep.tile([P, PACK, P], F32, name=f"w1_raw{t}_{s}") for t in range(TILES) for s in range(PASSES)}
         w2_raw = keep.tile([P, PACK, N], F32, name="w2_raw")
-        gates = keep.tile([P, D, V], F32, name="gates")
+        gates = [keep.tile([P, V], F32, name=f"gates{d}") for d in range(D)]
         plane = {}
 
-        nc.sync.dma_start(w1_raw0[:], w1_rows[0])
         for s in range(PASSES):
             for j0, n in pieces[s]:
                 x_t = keep.tile([P, n, T], F32, name=f"x{s}_{j0}")
                 nc.sync.dma_start(x_t[:], x_rows[s][:, j0 : j0 + n, :])
                 for j in range(n):
                     plane[s, j0 + j] = x_t[:, j, :]
-        for b in range(2):
-            nc.sync.dma_start(pairs[b][:], w1_rows[1][:, 2 * b : 2 * b + 2, :])
-        nc.sync.dma_start(gates[:], gate.rearrange("d p v -> p d v"))
-        for d, p in enumerate((pos1, pos2, pos3)):
-            nc.sync.dma_start(pos_t[d][:], p)
-        w2_rows = w2.rearrange("(g t r) m -> t g r m", t=PACK, r=8)
-        for t in range(PACK):
-            nc.sync.dma_start(w2_raw[:, t, :], w2_rows[t])
+            if s == 0:
+                for d, p in enumerate((pos1, pos2, pos3)):
+                    nc.sync.dma_start(pos_t[d][:], p)
+        for t in range(TILES):
+            for s in range(PASSES):
+                nc.sync.dma_start(w1_raw[t, s][:], w1_rows[s][:, :, t * P : (t + 1) * P])
+                if (t, s) == (1, 1):
+                    nc.sync.dma_start(gates[0][:], gate[0])
+                if (t, s) == (2, 0):
+                    for d in range(1, D):
+                        nc.sync.dma_start(gates[d][:], gate[d])
+        nc.sync.dma_start(w2_raw[:], w2.rearrange("(p j) m -> p j m", j=PACK))
+
+        ident = keep.tile([P, P], F32, name="ident")
+        make_identity(nc, ident[:])
 
         xg = [keep.tile([P, S, PACK], BF16, name=f"xg{s}", align_bytes=64) for s in range(PASSES)]
-        x_codes = [keep.tile([P, S], U32, name=f"x_codes{s}", align_bytes=64) for s in range(PASSES)]
+        sh = S // 2
+        x_codes = {}
         x_scales = [keep.tile([P, S], U8, name=f"x_scales{s}", align_bytes=64) for s in range(PASSES)]
-        w1g = [keep.tile([P, H * PACK], BF16, name=f"w1g{s}", align_bytes=64) for s in range(PASSES)]
-        w1_codes = [keep.tile([P, H], U32, name=f"w1_codes{s}", align_bytes=64) for s in range(PASSES)]
-        w1_scales = [keep.tile([P, H], U8, name=f"w1_scales{s}", align_bytes=64) for s in range(PASSES)]
+        w1g = {(t, s): keep.tile([P, P * PACK], BF16, name=f"w1g{t}_{s}", align_bytes=64) for t in range(TILES) for s in range(PASSES)}
+        w1_codes = [keep.tile([P, PASSES * P], U32, name=f"w1_codes{t}", align_bytes=64) for t in range(TILES)]
+        w1_scales = [keep.tile([P, PASSES * P], U8, name=f"w1_scales{t}", align_bytes=64) for t in range(TILES)]
 
         def quantize(codes, scales, grouped):
             nc.vector.quantize_mx(out=codes.bitcast(FP8X4), scales=scales, in_=grouped)
 
-        def quantize_x(s):
-            quantize(x_codes[s][:], x_scales[s][:], xg[s][:].rearrange("p n j -> p (n j)"))
+        def quantize_x(s, c0, c1):
+            quantize(x_codes[s, c0, c1], x_scales[s][:, c0:c1], xg[s][:, c0:c1, :].rearrange("p n j -> p (n j)"))
+
+        def quantize_w1(t, s):
+            quantize(w1_codes[t][:, s * P : (s + 1) * P], w1_scales[t][:, s * P : (s + 1) * P], w1g[t, s][:])
+
+        def interleave(dst, src):
+            return dst.rearrange("p (c i) j -> p c j i", i=4), src.rearrange("p j (c i) -> p c j i", i=4)
+
+        def lay_w1(t, s):
+            dst = w1g[t, s][:].rearrange("p (m j) -> p m j", j=PACK)
+            nc.scalar.copy(*interleave(dst, w1_raw[t, s][:]))
 
         picked = [
             keep.tile([P, PACK, S], F32, name="picked0", align_bytes=64),
             keep.tile([P, 2, S], F32, name="picked1", align_bytes=64),
         ]
-
-        def interleave(dst, src):
-            return dst.rearrange("p (c i) j -> p c j i", i=4), src.rearrange("p j (c i) -> p c j i", i=4)
-
-        def lay(engine_copy, raw, s, j0, j1, t0, t1):
-            engine_copy(
-                w1g[s][:].rearrange("p (t g r j) -> p t g r j", t=PACK, r=8, j=PACK)[:, t0:t1, :, :, j0:j1],
-                raw.rearrange("p j (g t r) -> p t g r j", t=PACK, r=8)[:, t0:t1],
-            )
-
-        lay(nc.scalar.copy, w1_raw0[:], 0, 0, PACK, 0, PACK)
         for j in range(PACK):
             nc.vector.tensor_copy(picked[0][:, j, :], plane[0, j].indirect(offs_t[:]))
-            if j == 1:
-                quantize(w1_codes[0][:], w1_scales[0][:], w1g[0][:])
         nc.scalar.copy(*interleave(xg[0][:], picked[0][:]))
         nc.vector.tensor_copy(picked[1][:, 0, :], plane[1, 0].indirect(offs_t[:]))
-        quantize_x(0)
+        codes0 = keep.tile([P, S], U32, name="x_codes0", align_bytes=64)
+        for c0, c1 in ((0, S), (0, sh), (sh, S)):
+            x_codes[0, c0, c1] = codes0[:, c0:c1]
+        quantize_x(0, 0, S)
         nc.vector.tensor_copy(picked[1][:, 1, :], plane[1, 1].indirect(offs_t[:]))
         nc.scalar.copy(*interleave(xg[1][:, :, 0:2], picked[1][:]))
         nc.vector.tensor_copy(xg[1][:, :, 2], plane[1, 2].indirect(offs_t[:]))
-        nc.vector.tensor_copy(xg[1][:, :, 3], plane[1, 3].indirect(offs_t[:]))
-        quantize_x(1)
-        lay(nc.scalar.copy, pairs[0][:], 1, 0, 2, 0, 1)
-        lay(nc.scalar.copy, pairs[0][:], 1, 0, 2, 1, PACK)
-        for t in range(PACK):
-            lay(nc.scalar.copy if t >= 2 else nc.vector.tensor_copy, pairs[1][:], 1, 2, 4, t, t + 1)
-            if t != 1 and t != 2:
-                continue
-            cols = slice((t - 1) * P, t * P)
-            quantize(w1_codes[1][:, cols], w1_scales[1][:, cols], w1g[1][:, (t - 1) * P * PACK : t * P * PACK])
-        for t in (2, 3):
-            cols = slice(t * P, (t + 1) * P)
-            quantize(w1_codes[1][:, cols], w1_scales[1][:, cols], w1g[1][:, t * P * PACK : (t + 1) * P * PACK])
+        lay_w1(0, 0)
+        lay_w1(0, 1)
+        nc.vector.tensor_copy(xg[1][:, 0:sh, 3], plane[1, 3].indirect(offs_t[:, 0 : sh // 16]))
+        nc.vector.tensor_copy(xg[1][:, sh:S, 3], plane[1, 3].indirect(offs_t[:, sh // 16 : S // 16]))
+        for s, c0 in enumerate((0, sh)):
+            quantize_w1(0, s)
+            codes1 = keep.tile([P, sh], U32, name=f"x_codes1_{c0}", tag=f"w1g0_{s}", align_bytes=64)
+            x_codes[1, c0, c0 + sh] = codes1[:]
+            quantize_x(1, c0, c0 + sh)
 
-        h = [keep.tile([P, S], F32, name=f"h{t}") for t in range(PACK)]
-        banks = []
-        for t in range(PACK):
-            w = S // 2 if t == 0 else S
-            banks.append([(c, w, psum.tile([P, w], F32, name=f"h_acc{t}_{c}")) for c in range(0, S, w)])
-        for s in range(PASSES):
-            for t in range(PACK):
-                for c, w, acc in banks[t]:
+        h = [keep.tile([P, S], F32, name=f"h{t}") for t in range(TILES)]
+        h_banks = [["hA", "hB"], ["hC", "hD"], ["hA", "hB"], ["hC", "hD"]]
+
+        def first_layer(t):
+            w = S // len(h_banks[t])
+            accs = [psum.tile([P, w], F32, name=f"h_acc{t}_{b}", tag=b) for b in h_banks[t]]
+            for s in range(PASSES):
+                for i, acc in enumerate(accs):
                     nc.tensor.matmul_mx(
                         out=acc[:],
-                        lhsT=w1_codes[s][:, t * P : (t + 1) * P].bitcast(FP8X4),
-                        lhsT_scale=w1_scales[s][:, t * P : (t + 1) * P],
-                        rhs=x_codes[s][:, c : c + w].bitcast(FP8X4),
-                        rhs_scale=x_scales[s][:, c : c + w],
+                        lhsT=w1_codes[t][:, s * P : (s + 1) * P].bitcast(FP8X4),
+                        lhsT_scale=w1_scales[t][:, s * P : (s + 1) * P],
+                        rhs=x_codes[s, i * w, (i + 1) * w].bitcast(FP8X4),
+                        rhs_scale=x_scales[s][:, i * w : (i + 1) * w],
                         start=(s == 0),
                         stop=(s == PASSES - 1),
                     )
-        for t in range(PACK):
-            for c, w, acc in banks[t]:
-                if c == 0:
-                    nc.scalar.activation(h[t][:, c : c + w], acc[:], RELU)
+            for i, acc in enumerate(accs):
+                if i == 0 or t > 0:
+                    nc.scalar.activation(h[t][:, i * w : (i + 1) * w], acc[:], RELU)
                 else:
-                    nc.vector.tensor_scalar_max(h[t][:, c : c + w], acc[:], 0.0)
+                    nc.vector.tensor_scalar_max(h[t][:, i * w : (i + 1) * w], acc[:], 0.0)
 
-        u = [keep.tile([P, PACK, V], F32, name=f"u{d}") for d in range(D)]
-        s01 = keep.tile([P, PACK, V], F32, name="s01")
+        def prepare(t):
+            lay_w1(t, 0)
+            lay_w1(t, 1)
+            quantize_w1(t, 0)
+            quantize_w1(t, 1)
+
+        halves = V // P
+        u = {}
+        reuse = {(0, 0): (1, "u0"), (0, 1): (1, "w1g2_0"), (0, 2): (1, "w1g2_1"), (1, 0): (1, "w1g3_0"), (1, 1): (5, "w1g3_1"), (3, 0): (3, "u3")}
+        zt = []
         w2g = keep.tile([P, N, PACK], BF16, name="w2g", align_bytes=64)
         w2_codes = keep.tile([P, N], U32, name="w2_codes", align_bytes=64)
         w2_scales = keep.tile([P, N], U8, name="w2_scales", align_bytes=64)
-        nc.scalar.copy(*interleave(w2g[:], w2_raw[:]))
-        vh = V // 2
 
         def fetch(t, d, v0, v1):
-            nc.vector.tensor_tensor(u[d][:, t, v0:v1], h[t][:].indirect(pos_t[d][:, v0 // 16 : v1 // 16]), gates[:, d, v0:v1], MULT)
+            if v0 == 0 and (t, d) in reuse:
+                n, tag = reuse[t, d]
+                terms = keep.tile([P, n, V], F32, name=f"u{t}_{d}", tag=tag, align_bytes=64)
+                for i in range(n):
+                    u[divmod(D * t + d + i, D)] = terms[:, i, :]
+            nc.vector.tensor_tensor(u[t, d][:, v0:v1], h[t][:].indirect(pos_t[d][:, v0 // 16 : v1 // 16]), gates[d][:, v0:v1], MULT)
 
-        def add_pair(t):
-            pair = slice(t, t + 2)
-            nc.vector.tensor_tensor(s01[:, pair, :], u[0][:, pair, :], u[1][:, pair, :], ADD)
+        def turn_and_add(t, d, c, acc):
+            nc.tensor.matmul(acc, u[t, d][:, c * P : (c + 1) * P], ident[:], start=(d == 0), stop=(d == D - 1), is_transpose=True)
 
-        for t in range(PACK - 1):
+        def z_banks(t):
+            return [psum.tile([P, P], F32, name=f"z_acc{t}_{c}", tag=f"z{t % 2}_{c}") for c in range(halves)]
+
+        def round_z(copy, t, c, acc):
+            copy(zt[c][:, :, 32 * t : 32 * (t + 1), :], acc.rearrange("v (q a e) -> v a q e", a=2, e=2))
+
+        prepare(1)
+        first_layer(0)
+        first_layer(1)
+        prepare(2)
+        lay_w1(3, 0)
+        lay_w1(3, 1)
+        nc.scalar.copy(*interleave(w2g[:], w2_raw[:]))
+        for c, tag in enumerate(("w1_raw3_1", "w2_raw")):
+            zt.append(keep.tile([P, 2, P, 2], BF16, name=f"zt{c}", tag=tag))
+        for t in range(TILES - 1):
+            if t == 1:
+                quantize_w1(3, 0)
+                quantize_w1(3, 1)
+            if t + 2 < TILES:
+                first_layer(t + 2)
+            accs = z_banks(t)
             for d in range(D):
                 fetch(t, d, 0, V)
-            if t == 1:
-                add_pair(0)
+                for c in range(halves):
+                    turn_and_add(t, d, c, accs[c][:])
+            if t == TILES - 2:
                 quantize(w2_codes[:], w2_scales[:], w2g[:].rearrange("p m j -> p (m j)"))
-        fetch(PACK - 1, 0, 0, V)
-        fetch(PACK - 1, 1, 0, V)
-        fetch(PACK - 1, 2, 0, vh)
-        add_pair(2)
-        fetch(PACK - 1, 2, vh, V)
-
-        zg = keep.tile([P, V, PACK], BF16, name="zg", align_bytes=64)
-        z_codes = keep.tile([P, V], U32, name="z_codes", align_bytes=64)
-        z_scales = keep.tile([P, V], U8, name="z_scales", align_bytes=64)
-        for c in (0, vh):
-            nc.vector.tensor_tensor(
-                *interleave(zg[:, c : c + vh, :], s01[:, :, c : c + vh]),
-                u[2][:, :, c : c + vh].rearrange("p t (c i) -> p c t i", i=4),
-                ADD,
-            )
-        for c in (0, vh):
-            quantize(z_codes[:, c : c + vh], z_scales[:, c : c + vh], zg[:, c : c + vh, :].rearrange("p v j -> p (v j)"))
-        for c in (0, vh):
-            acc = psum.tile([P, vh], F32, name=f"o_acc{c}")
+            for c in range(halves):
+                round_z(nc.scalar.copy, t, c, accs[c][:])
+        last = TILES - 1
+        accs = z_banks(last)
+        for c in range(halves):
+            for d in range(D):
+                fetch(last, d, c * P, (c + 1) * P)
+                turn_and_add(last, d, c, accs[c][:])
+        for c in range(halves):
+            copy = nc.scalar.copy if c == 0 else nc.vector.tensor_copy
+            round_z(copy, last, c, accs[c][:])
+            back = psum.tile([P, 2, P], F32, name=f"back{c}", tag=("hA", "hB")[c])
+            words = zt[c][:].rearrange("v a p e -> v (a p e)").bitcast(F32)
+            for a in range(2):
+                nc.tensor.transpose(back[:, a, :], words[:, a * P : (a + 1) * P], ident[:])
+            zg = keep.tile([P, P * PACK], BF16, name=f"zg{c}", align_bytes=64)
+            copy(zg[:].bitcast(F32).rearrange("p (v a) -> p v a", a=2), back[:].rearrange("p a v -> p v a"))
+            z_codes = keep.tile([P, P], U32, name=f"z_codes{c}", align_bytes=64)
+            z_scales = keep.tile([P, P], U8, name=f"z_scales{c}", align_bytes=64)
+            quantize(z_codes[:], z_scales[:], zg[:])
+            o_acc = psum.tile([P, P], F32, name=f"o_acc{c}", tag=("hC", "hD")[c])
             nc.tensor.matmul_mx(
-                out=acc[:],
+                out=o_acc[:],
                 lhsT=w2_codes[:].bitcast(FP8X4),
                 lhsT_scale=w2_scales[:],
-                rhs=z_codes[:, c : c + vh].bitcast(FP8X4),
-                rhs_scale=z_scales[:, c : c + vh],
+                rhs=z_codes[:].bitcast(FP8X4),
+                rhs_scale=z_scales[:],
                 start=True,
                 stop=True,
             )
-            res = keep.tile([P, vh], F32, name=f"res{c}")
-            if c == 0:
-                nc.scalar.copy(res[:], acc[:])
-            else:
-                nc.vector.tensor_copy(res[:], acc[:])
-            nc.sync.dma_start(out[:, c : c + vh], res[:])
+            res = keep.tile([P, P], F32, name=f"res{c}")
+            copy(res[:], o_acc[:])
+            nc.sync.dma_start(out[:, c * P : (c + 1) * P], res[:])

@@ -33,9 +33,9 @@ def tile_picked_sage_relu_e_kernel(tc, xT, w1, w2, gate, offs, pos1, pos2, pos3,
         x_rows = xT.rearrange("(s p j) t -> s p j t", p=P, j=PACK)
         w1_rows = w1.rearrange("(s p j) c -> s p j c", p=P, j=PACK)
         pieces = [[(0, 2), (2, 2)], [(0, 1), (1, 1), (2, 1), (3, 1)]]
-        w1_raw = {(t, s): keep.tile([P, PACK, P], F32, name=f"w1_raw{t}_{s}") for t in range(TILES) for s in range(PASSES)}
-        w2_raw = keep.tile([P, PACK, N], F32, name="w2_raw")
-        gates = [keep.tile([P, V], F32, name=f"gates{d}") for d in range(D)]
+        w1_raw = {(t, s): keep.tile([P, PACK, P], F32, name=f"w1_raw{t}_{s}", align_bytes=64) for t in range(TILES) for s in range(PASSES)}
+        w2_raw = keep.tile([P, PACK, N], F32, name="w2_raw", align_bytes=64)
+        gates = [keep.tile([P, V], F32, name=f"gates{d}", align_bytes=64) for d in range(D)]
         plane = {}
 
         for s in range(PASSES):
@@ -50,15 +50,25 @@ def tile_picked_sage_relu_e_kernel(tc, xT, w1, w2, gate, offs, pos1, pos2, pos3,
         for t in range(TILES):
             for s in range(PASSES):
                 nc.sync.dma_start(w1_raw[t, s][:], w1_rows[s][:, :, t * P : (t + 1) * P])
-                if (t, s) == (1, 1):
-                    nc.sync.dma_start(gates[0][:], gate[0])
-                if (t, s) == (2, 0):
-                    for d in range(1, D):
-                        nc.sync.dma_start(gates[d][:], gate[d])
         nc.sync.dma_start(w2_raw[:], w2.rearrange("(p j) m -> p j m", j=PACK))
 
         ident = keep.tile([P, P], F32, name="ident")
         make_identity(nc, ident[:])
+
+        halves = V // P
+        gate_rows = keep.tile([P, V], F32, name="gate_rows")
+        nc.gpsimd.memset(gate_rows[:], 0.0)
+        nc.gpsimd.dma_start(gate_rows[0:D, :], gate[:, 0, :])
+        turned = psum.tile([P, halves, P], F32, name="gate_turned", tag="hA")
+        for c in range(halves):
+            nc.tensor.transpose(turned[:, c, :], gate_rows[:, c * P : (c + 1) * P], ident[:])
+        gate_cols = keep.tile([P, halves, D], F32, name="gate_cols")
+        nc.scalar.copy(gate_cols[:], turned[:, :, 0:D])
+        for d, bank in enumerate(("hB", "hC", "hD")):
+            spread = psum.tile([P, halves, P], F32, name=f"gate_spread{d}", tag=bank)
+            for c in range(halves):
+                nc.tensor.transpose(spread[:, c, :], gate_cols[:, c, d : d + 1].to_broadcast([P, P]), ident[:])
+            nc.scalar.copy(gates[d][:], spread[:].rearrange("p c v -> p (c v)"))
 
         xg = [keep.tile([P, S, PACK], BF16, name=f"xg{s}", align_bytes=64) for s in range(PASSES)]
         sh = S // 2
@@ -103,14 +113,15 @@ def tile_picked_sage_relu_e_kernel(tc, xT, w1, w2, gate, offs, pos1, pos2, pos3,
         lay_w1(0, 1)
         nc.vector.tensor_copy(xg[1][:, 0:sh, 3], plane[1, 3].indirect(offs_t[:, 0 : sh // 16]))
         nc.vector.tensor_copy(xg[1][:, sh:S, 3], plane[1, 3].indirect(offs_t[:, sh // 16 : S // 16]))
+        codes1 = keep.tile([P, S], U32, name="x_codes1", tag="w1_raw0_0", align_bytes=64)
+        for c0, c1 in ((0, S), (0, sh), (sh, S)):
+            x_codes[1, c0, c1] = codes1[:, c0:c1]
         for s, c0 in enumerate((0, sh)):
             quantize_w1(0, s)
-            codes1 = keep.tile([P, sh], U32, name=f"x_codes1_{c0}", tag=f"w1g0_{s}", align_bytes=64)
-            x_codes[1, c0, c0 + sh] = codes1[:]
             quantize_x(1, c0, c0 + sh)
 
         h = [keep.tile([P, S], F32, name=f"h{t}") for t in range(TILES)]
-        h_banks = [["hA", "hB"], ["hC", "hD"], ["hA", "hB"], ["hC", "hD"]]
+        h_banks = [["hA", "hB"], ["hC"], ["hD"], ["hA"]]
 
         def first_layer(t):
             w = S // len(h_banks[t])
@@ -138,12 +149,10 @@ def tile_picked_sage_relu_e_kernel(tc, xT, w1, w2, gate, offs, pos1, pos2, pos3,
             quantize_w1(t, 0)
             quantize_w1(t, 1)
 
-        halves = V // P
         u = {}
-        reuse = {(0, 0): (1, "u0"), (0, 1): (1, "w1g2_0"), (0, 2): (1, "w1g2_1"), (1, 0): (1, "w1g3_0"), (1, 1): (5, "w1g3_1"), (3, 0): (3, "u3")}
+        reuse = {(0, 0): (1, "u0"), (0, 1): (1, "w1_raw2_0"), (0, 2): (2, "w1_raw2_1"), (1, 1): (1, "w1_raw3_0"), (1, 2): (1, "w1_raw3_1"), (2, 0): (6, "u2")}
         zt = []
         w2g = keep.tile([P, N, PACK], BF16, name="w2g", align_bytes=64)
-        w2_codes = keep.tile([P, N], U32, name="w2_codes", align_bytes=64)
         w2_scales = keep.tile([P, N], U8, name="w2_scales", align_bytes=64)
 
         def fetch(t, d, v0, v1):
@@ -154,11 +163,9 @@ def tile_picked_sage_relu_e_kernel(tc, xT, w1, w2, gate, offs, pos1, pos2, pos3,
                     u[divmod(D * t + d + i, D)] = terms[:, i, :]
             nc.vector.tensor_tensor(u[t, d][:, v0:v1], h[t][:].indirect(pos_t[d][:, v0 // 16 : v1 // 16]), gates[d][:, v0:v1], MULT)
 
-        def turn_and_add(t, d, c, acc):
-            nc.tensor.matmul(acc, u[t, d][:, c * P : (c + 1) * P], ident[:], start=(d == 0), stop=(d == D - 1), is_transpose=True)
-
-        def z_banks(t):
-            return [psum.tile([P, P], F32, name=f"z_acc{t}_{c}", tag=f"z{t % 2}_{c}") for c in range(halves)]
+        def turn_and_add(t, c, acc, turns):
+            for i, d in enumerate(turns):
+                nc.tensor.matmul(acc, u[t, d][:, c * P : (c + 1) * P], ident[:], start=(i == 0), stop=(i == D - 1), is_transpose=True)
 
         def round_z(copy, t, c, acc):
             copy(zt[c][:, :, 32 * t : 32 * (t + 1), :], acc.rearrange("v (q a e) -> v a q e", a=2, e=2))
@@ -167,36 +174,38 @@ def tile_picked_sage_relu_e_kernel(tc, xT, w1, w2, gate, offs, pos1, pos2, pos3,
         first_layer(0)
         first_layer(1)
         prepare(2)
-        lay_w1(3, 0)
-        lay_w1(3, 1)
+        prepare(3)
+        first_layer(2)
+        first_layer(3)
         nc.scalar.copy(*interleave(w2g[:], w2_raw[:]))
-        for c, tag in enumerate(("w1_raw3_1", "w2_raw")):
-            zt.append(keep.tile([P, 2, P, 2], BF16, name=f"zt{c}", tag=tag))
-        for t in range(TILES - 1):
-            if t == 1:
-                quantize_w1(3, 0)
-                quantize_w1(3, 1)
-            if t + 2 < TILES:
-                first_layer(t + 2)
-            accs = z_banks(t)
+        for c, tag in enumerate(("w2_raw", "w1g3_1")):
+            zt.append(keep.tile([P, 2, P, 2], BF16, name=f"zt{c}", tag=tag, align_bytes=64))
+        last = TILES - 1
+        for t in range(last - 1):
             for d in range(D):
                 fetch(t, d, 0, V)
-                for c in range(halves):
-                    turn_and_add(t, d, c, accs[c][:])
-            if t == TILES - 2:
-                quantize(w2_codes[:], w2_scales[:], w2g[:].rearrange("p m j -> p (m j)"))
+            acc = psum.tile([P, halves, P], F32, name=f"z_acc{t}", tag=f"z{t % 2}")
             for c in range(halves):
-                round_z(nc.scalar.copy, t, c, accs[c][:])
-        last = TILES - 1
-        accs = z_banks(last)
+                turn_and_add(t, c, acc[:, c, :], (2, 1, 0))
+            for c in range(halves):
+                round_z(nc.scalar.copy, t, c, acc[:, c, :])
+        accs = [psum.tile([P, P], F32, name=f"z_acc{last - 1}_{c}", tag=("hB", "hC")[c]) for c in range(halves)]
+        for d in range(D):
+            fetch(last - 1, d, 0, V)
+        for c in range(halves):
+            turn_and_add(last - 1, c, accs[c][:], (0, 1, 2))
+            round_z(nc.scalar.copy, last - 1, c, accs[c][:])
+        accs = [psum.tile([P, P], F32, name=f"z_acc{last}_{c}", tag=f"z{2 + c}") for c in range(halves)]
         for c in range(halves):
             for d in range(D):
                 fetch(last, d, c * P, (c + 1) * P)
-                turn_and_add(last, d, c, accs[c][:])
+            turn_and_add(last, c, accs[c][:], (0, 1, 2))
+        w2_codes = keep.tile([P, N], U32, name="w2_codes", tag=f"gates{D - 1}", align_bytes=64)
+        quantize(w2_codes[:], w2_scales[:], w2g[:].rearrange("p m j -> p (m j)"))
         for c in range(halves):
             copy = nc.scalar.copy if c == 0 else nc.vector.tensor_copy
             round_z(copy, last, c, accs[c][:])
-            back = psum.tile([P, 2, P], F32, name=f"back{c}", tag=("hA", "hB")[c])
+            back = psum.tile([P, 2, P], F32, name=f"back{c}", tag=("hD", "z0")[c])
             words = zt[c][:].rearrange("v a p e -> v (a p e)").bitcast(F32)
             for a in range(2):
                 nc.tensor.transpose(back[:, a, :], words[:, a * P : (a + 1) * P], ident[:])
@@ -205,7 +214,7 @@ def tile_picked_sage_relu_e_kernel(tc, xT, w1, w2, gate, offs, pos1, pos2, pos3,
             z_codes = keep.tile([P, P], U32, name=f"z_codes{c}", align_bytes=64)
             z_scales = keep.tile([P, P], U8, name=f"z_scales{c}", align_bytes=64)
             quantize(z_codes[:], z_scales[:], zg[:])
-            o_acc = psum.tile([P, P], F32, name=f"o_acc{c}", tag=("hC", "hD")[c])
+            o_acc = psum.tile([P, P], F32, name=f"o_acc{c}", tag=("hA", "z1")[c])
             nc.tensor.matmul_mx(
                 out=o_acc[:],
                 lhsT=w2_codes[:].bitcast(FP8X4),

@@ -58,17 +58,7 @@ def tile_picked_sage_relu_e_kernel(tc, xT, w1, w2, gate, offs, pos1, pos2, pos3,
         halves = V // P
         gate_rows = keep.tile([P, V], F32, name="gate_rows")
         nc.gpsimd.memset(gate_rows[:], 0.0)
-        nc.gpsimd.dma_start(gate_rows[0:D, :], gate[:, 0, :])
-        turned = psum.tile([P, halves, P], F32, name="gate_turned", tag="hA")
-        for c in range(halves):
-            nc.tensor.transpose(turned[:, c, :], gate_rows[:, c * P : (c + 1) * P], ident[:])
-        gate_cols = keep.tile([P, halves, D], F32, name="gate_cols")
-        nc.scalar.copy(gate_cols[:], turned[:, :, 0:D])
-        for d, bank in enumerate(("hB", "hC", "hD")):
-            spread = psum.tile([P, halves, P], F32, name=f"gate_spread{d}", tag=bank)
-            for c in range(halves):
-                nc.tensor.transpose(spread[:, c, :], gate_cols[:, c, d : d + 1].to_broadcast([P, P]), ident[:])
-            nc.scalar.copy(gates[d][:], spread[:].rearrange("p c v -> p (c v)"))
+        nc.scalar.dma_start(gate_rows[0:D, :], gate[:, 0, :])
 
         xg = [keep.tile([P, S, PACK], BF16, name=f"xg{s}", align_bytes=64) for s in range(PASSES)]
         sh = S // 2
@@ -101,6 +91,16 @@ def tile_picked_sage_relu_e_kernel(tc, xT, w1, w2, gate, offs, pos1, pos2, pos3,
         for j in range(PACK):
             nc.vector.tensor_copy(picked[0][:, j, :], plane[0, j].indirect(offs_t[:]))
         nc.scalar.copy(*interleave(xg[0][:], picked[0][:]))
+        turned = psum.tile([P, halves, P], F32, name="gate_turned", tag="hA")
+        for c in range(halves):
+            nc.tensor.transpose(turned[:, c, :], gate_rows[:, c * P : (c + 1) * P], ident[:])
+        gate_cols = keep.tile([P, halves, D], F32, name="gate_cols", tag="picked0", align_bytes=64)
+        nc.scalar.copy(gate_cols[:], turned[:, :, 0:D])
+        for d, bank in enumerate(("hB", "hC", "hD")):
+            spread = psum.tile([P, halves, P], F32, name=f"gate_spread{d}", tag=bank)
+            for c in range(halves):
+                nc.tensor.transpose(spread[:, c, :], gate_cols[:, c, d : d + 1].to_broadcast([P, P]), ident[:])
+            nc.scalar.copy(gates[d][:], spread[:].rearrange("p c v -> p (c v)"))
         nc.vector.tensor_copy(picked[1][:, 0, :], plane[1, 0].indirect(offs_t[:]))
         codes0 = keep.tile([P, S], U32, name="x_codes0", align_bytes=64)
         for c0, c1 in ((0, S), (0, sh), (sh, S)):

@@ -28,7 +28,6 @@ def tile_picked_sage_relu_e_kernel(tc, xT, w1, w2, gate, offs, pos1, pos2, pos3,
 
         offs_t = keep.tile([P, S // 16], U16, name="offs_t")
         pos_t = [keep.tile([P, V // 16], U16, name=f"pos_t{d}") for d in range(D)]
-        nc.sync.dma_start(offs_t[:], offs)
 
         x_rows = xT.rearrange("(s p j) t -> s p j t", p=P, j=PACK)
         w1_rows = w1.rearrange("(s p j) c -> s p j c", p=P, j=PACK)
@@ -42,6 +41,8 @@ def tile_picked_sage_relu_e_kernel(tc, xT, w1, w2, gate, offs, pos1, pos2, pos3,
             for j0, n in pieces[s]:
                 x_t = keep.tile([P, n, T], F32, name=f"x{s}_{j0}")
                 nc.sync.dma_start(x_t[:], x_rows[s][:, j0 : j0 + n, :])
+                if (s, j0) == (0, 0):
+                    nc.sync.dma_start(offs_t[:], offs)
                 for j in range(n):
                     plane[s, j0 + j] = x_t[:, j, :]
             if s == 0:
@@ -82,7 +83,8 @@ def tile_picked_sage_relu_e_kernel(tc, xT, w1, w2, gate, offs, pos1, pos2, pos3,
 
         def lay_w1(t, s):
             dst = w1g[t, s][:].rearrange("p (m j) -> p m j", j=PACK)
-            nc.scalar.copy(*interleave(dst, w1_raw[t, s][:]))
+            copy = nc.vector.tensor_copy if (t, s) == (1, 1) else nc.scalar.copy
+            copy(*interleave(dst, w1_raw[t, s][:]))
 
         picked = [
             keep.tile([P, PACK, S], F32, name="picked0", align_bytes=64),

@@ -32,14 +32,14 @@ def tile_picked_sage_relu_e_kernel(tc, xT, w1, w2, gate, offs, pos1, pos2, pos3,
         x_rows = xT.rearrange("(s p j) t -> s p j t", p=P, j=PACK)
         w1_rows = w1.rearrange("(s p j) c -> s p j c", p=P, j=PACK)
         pieces = [[(0, 2), (2, 2)], [(0, 1), (1, 1), (2, 1), (3, 1)]]
-        w1_raw = {(t, s): keep.tile([P, PACK, P], F32, name=f"w1_raw{t}_{s}", align_bytes=64) for t in range(TILES) for s in range(PASSES)}
-        w2_raw = keep.tile([P, PACK, N], F32, name="w2_raw", align_bytes=64)
-        gates = [keep.tile([P, V], F32, name=f"gates{d}", align_bytes=64) for d in range(D)]
+        w1_raw = {(t, s): keep.tile([P, PACK, P], F32, name=f"w1_raw{t}_{s}", align_bytes=256) for t in range(TILES) for s in range(PASSES)}
+        w2_raw = keep.tile([P, PACK, N], F32, name="w2_raw", align_bytes=256)
+        gates = [keep.tile([P, V], F32, name=f"gates{d}", align_bytes=256) for d in range(D)]
         plane = {}
 
         for s in range(PASSES):
             for j0, n in pieces[s]:
-                x_t = keep.tile([P, n, T], F32, name=f"x{s}_{j0}")
+                x_t = keep.tile([P, n, T], F32, name=f"x{s}_{j0}", align_bytes=256)
                 nc.sync.dma_start(x_t[:], x_rows[s][:, j0 : j0 + n, :])
                 if (s, j0) == (0, 0):
                     nc.sync.dma_start(offs_t[:], offs)
@@ -61,13 +61,13 @@ def tile_picked_sage_relu_e_kernel(tc, xT, w1, w2, gate, offs, pos1, pos2, pos3,
         nc.gpsimd.memset(gate_rows[:], 0.0)
         nc.scalar.dma_start(gate_rows[0:D, :], gate[:, 0, :])
 
-        xg = [keep.tile([P, S, PACK], BF16, name=f"xg{s}", align_bytes=64) for s in range(PASSES)]
+        xg = [keep.tile([P, S, PACK], BF16, name=f"xg{s}", align_bytes=256) for s in range(PASSES)]
         sh = S // 2
         x_codes = {}
-        x_scales = [keep.tile([P, S], U8, name=f"x_scales{s}", align_bytes=64) for s in range(PASSES)]
-        w1g = {(t, s): keep.tile([P, P * PACK], BF16, name=f"w1g{t}_{s}", align_bytes=64) for t in range(TILES) for s in range(PASSES)}
-        w1_codes = [keep.tile([P, PASSES * P], U32, name=f"w1_codes{t}", align_bytes=64) for t in range(TILES)]
-        w1_scales = [keep.tile([P, PASSES * P], U8, name=f"w1_scales{t}", align_bytes=64) for t in range(TILES)]
+        x_scales = [keep.tile([P, S], U8, name=f"x_scales{s}", align_bytes=256) for s in range(PASSES)]
+        w1g = {(t, s): keep.tile([P, P * PACK], BF16, name=f"w1g{t}_{s}", align_bytes=256) for t in range(TILES) for s in range(PASSES)}
+        w1_codes = [keep.tile([P, PASSES * P], U32, name=f"w1_codes{t}", align_bytes=256) for t in range(TILES)]
+        w1_scales = [keep.tile([P, PASSES * P], U8, name=f"w1_scales{t}", align_bytes=256) for t in range(TILES)]
 
         def quantize(codes, scales, grouped):
             nc.vector.quantize_mx(out=codes.bitcast(FP8X4), scales=scales, in_=grouped)
@@ -87,8 +87,8 @@ def tile_picked_sage_relu_e_kernel(tc, xT, w1, w2, gate, offs, pos1, pos2, pos3,
             copy(*interleave(dst, w1_raw[t, s][:]))
 
         picked = [
-            keep.tile([P, PACK, S], F32, name="picked0", align_bytes=64),
-            keep.tile([P, 2, S], F32, name="picked1", align_bytes=64),
+            keep.tile([P, PACK, S], F32, name="picked0", align_bytes=256),
+            keep.tile([P, 2, S], F32, name="picked1", align_bytes=256),
         ]
         for j in range(PACK):
             nc.vector.tensor_copy(picked[0][:, j, :], plane[0, j].indirect(offs_t[:]))
@@ -96,7 +96,7 @@ def tile_picked_sage_relu_e_kernel(tc, xT, w1, w2, gate, offs, pos1, pos2, pos3,
         turned = psum.tile([P, halves, P], F32, name="gate_turned", tag="hA")
         for c in range(halves):
             nc.tensor.transpose(turned[:, c, :], gate_rows[:, c * P : (c + 1) * P], ident[:])
-        gate_cols = keep.tile([P, halves, D], F32, name="gate_cols", tag="picked0", align_bytes=64)
+        gate_cols = keep.tile([P, halves, D], F32, name="gate_cols", tag="picked0", align_bytes=256)
         nc.scalar.copy(gate_cols[:], turned[:, :, 0:D])
         for d, bank in enumerate(("hB", "hC", "hD")):
             spread = psum.tile([P, halves, P], F32, name=f"gate_spread{d}", tag=bank)
@@ -104,7 +104,7 @@ def tile_picked_sage_relu_e_kernel(tc, xT, w1, w2, gate, offs, pos1, pos2, pos3,
                 nc.tensor.transpose(spread[:, c, :], gate_cols[:, c, d : d + 1].to_broadcast([P, P]), ident[:])
             nc.scalar.copy(gates[d][:], spread[:].rearrange("p c v -> p (c v)"))
         nc.vector.tensor_copy(picked[1][:, 0, :], plane[1, 0].indirect(offs_t[:]))
-        codes0 = keep.tile([P, S], U32, name="x_codes0", align_bytes=64)
+        codes0 = keep.tile([P, S], U32, name="x_codes0", align_bytes=256)
         for c0, c1 in ((0, S), (0, sh), (sh, S)):
             x_codes[0, c0, c1] = codes0[:, c0:c1]
         quantize_x(0, 0, S)
@@ -115,14 +115,14 @@ def tile_picked_sage_relu_e_kernel(tc, xT, w1, w2, gate, offs, pos1, pos2, pos3,
         lay_w1(0, 1)
         nc.vector.tensor_copy(xg[1][:, 0:sh, 3], plane[1, 3].indirect(offs_t[:, 0 : sh // 16]))
         nc.vector.tensor_copy(xg[1][:, sh:S, 3], plane[1, 3].indirect(offs_t[:, sh // 16 : S // 16]))
-        codes1 = keep.tile([P, S], U32, name="x_codes1", tag="w1_raw0_0", align_bytes=64)
+        codes1 = keep.tile([P, S], U32, name="x_codes1", tag="w1_raw0_0", align_bytes=256)
         for c0, c1 in ((0, S), (0, sh), (sh, S)):
             x_codes[1, c0, c1] = codes1[:, c0:c1]
         for s, c0 in enumerate((0, sh)):
             quantize_w1(0, s)
             quantize_x(1, c0, c0 + sh)
 
-        h = [keep.tile([P, S], F32, name=f"h{t}") for t in range(TILES)]
+        h = [keep.tile([P, S], F32, name=f"h{t}", align_bytes=256) for t in range(TILES)]
         h_banks = [["hA", "hB"], ["hC"], ["hD"], ["hA"]]
 
         def first_layer(t):
@@ -154,13 +154,13 @@ def tile_picked_sage_relu_e_kernel(tc, xT, w1, w2, gate, offs, pos1, pos2, pos3,
         u = {}
         reuse = {(0, 0): (1, "u0"), (0, 1): (1, "w1_raw2_0"), (0, 2): (2, "w1_raw2_1"), (1, 1): (1, "w1_raw3_0"), (1, 2): (1, "w1_raw3_1"), (2, 0): (6, "u2")}
         zt = []
-        w2g = keep.tile([P, N, PACK], BF16, name="w2g", align_bytes=64)
-        w2_scales = keep.tile([P, N], U8, name="w2_scales", align_bytes=64)
+        w2g = keep.tile([P, N, PACK], BF16, name="w2g", align_bytes=256)
+        w2_scales = keep.tile([P, N], U8, name="w2_scales", align_bytes=256)
 
         def fetch(t, d, v0, v1):
             if v0 == 0 and (t, d) in reuse:
                 n, tag = reuse[t, d]
-                terms = keep.tile([P, n, V], F32, name=f"u{t}_{d}", tag=tag, align_bytes=64)
+                terms = keep.tile([P, n, V], F32, name=f"u{t}_{d}", tag=tag, align_bytes=256)
                 for i in range(n):
                     u[divmod(D * t + d + i, D)] = terms[:, i, :]
             nc.vector.tensor_tensor(u[t, d][:, v0:v1], h[t][:].indirect(pos_t[d][:, v0 // 16 : v1 // 16]), gates[d][:, v0:v1], MULT)
@@ -181,7 +181,7 @@ def tile_picked_sage_relu_e_kernel(tc, xT, w1, w2, gate, offs, pos1, pos2, pos3,
         first_layer(3)
         nc.scalar.copy(*interleave(w2g[:], w2_raw[:]))
         for c, tag in enumerate(("w2_raw", "w1g3_1")):
-            zt.append(keep.tile([P, 2, P, 2], BF16, name=f"zt{c}", tag=tag, align_bytes=64))
+            zt.append(keep.tile([P, 2, P, 2], BF16, name=f"zt{c}", tag=tag, align_bytes=256))
         last = TILES - 1
         for t in range(last - 1):
             for d in range(D):
@@ -202,7 +202,7 @@ def tile_picked_sage_relu_e_kernel(tc, xT, w1, w2, gate, offs, pos1, pos2, pos3,
             for d in range(D):
                 fetch(last, d, c * P, (c + 1) * P)
             turn_and_add(last, c, accs[c][:], (0, 1, 2))
-        w2_codes = keep.tile([P, N], U32, name="w2_codes", tag=f"gates{D - 1}", align_bytes=64)
+        w2_codes = keep.tile([P, N], U32, name="w2_codes", tag=f"gates{D - 1}", align_bytes=256)
         quantize(w2_codes[:], w2_scales[:], w2g[:].rearrange("p m j -> p (m j)"))
         for c in range(halves):
             copy = nc.scalar.copy if c == 0 else nc.vector.tensor_copy
@@ -211,10 +211,10 @@ def tile_picked_sage_relu_e_kernel(tc, xT, w1, w2, gate, offs, pos1, pos2, pos3,
             words = zt[c][:].rearrange("v a p e -> v (a p e)").bitcast(F32)
             for a in range(2):
                 nc.tensor.transpose(back[:, a, :], words[:, a * P : (a + 1) * P], ident[:])
-            zg = keep.tile([P, P * PACK], BF16, name=f"zg{c}", align_bytes=64)
+            zg = keep.tile([P, P * PACK], BF16, name=f"zg{c}", align_bytes=256)
             copy(zg[:].bitcast(F32).rearrange("p (v a) -> p v a", a=2), back[:].rearrange("p a v -> p v a"))
-            z_codes = keep.tile([P, P], U32, name=f"z_codes{c}", align_bytes=64)
-            z_scales = keep.tile([P, P], U8, name=f"z_scales{c}", align_bytes=64)
+            z_codes = keep.tile([P, P], U32, name=f"z_codes{c}", align_bytes=256)
+            z_scales = keep.tile([P, P], U8, name=f"z_scales{c}", align_bytes=256)
             quantize(z_codes[:], z_scales[:], zg[:])
             o_acc = psum.tile([P, P], F32, name=f"o_acc{c}", tag=("hA", "z1")[c])
             nc.tensor.matmul_mx(
@@ -226,6 +226,6 @@ def tile_picked_sage_relu_e_kernel(tc, xT, w1, w2, gate, offs, pos1, pos2, pos3,
                 start=True,
                 stop=True,
             )
-            res = keep.tile([P, P], F32, name=f"res{c}")
+            res = keep.tile([P, P], F32, name=f"res{c}", align_bytes=256)
             copy(res[:], o_acc[:])
             nc.sync.dma_start(out[:, c * P : (c + 1) * P], res[:])

@@ -105,7 +105,8 @@ def tile_picked_sage_relu_e_kernel(tc, xT, w1, w2, gate, offs, pos1, pos2, pos3,
             nc.scalar.copy(gates[d][:], spread[:].rearrange("p c v -> p (c v)"))
         nc.vector.tensor_copy(picked[1][:, 0, :], plane[1, 0].indirect(offs_t[:]))
         codes0 = keep.tile([P, S], U32, name="x_codes0", align_bytes=256)
-        for c0, c1 in ((0, S), (0, sh), (sh, S)):
+        parts = tuple((c, c + P) for c in range(0, S, P))
+        for c0, c1 in ((0, S),) + parts:
             x_codes[0, c0, c1] = codes0[:, c0:c1]
         quantize_x(0, 0, S)
         nc.vector.tensor_copy(picked[1][:, 1, :], plane[1, 1].indirect(offs_t[:]))
@@ -116,34 +117,34 @@ def tile_picked_sage_relu_e_kernel(tc, xT, w1, w2, gate, offs, pos1, pos2, pos3,
         nc.vector.tensor_copy(xg[1][:, 0:sh, 3], plane[1, 3].indirect(offs_t[:, 0 : sh // 16]))
         nc.vector.tensor_copy(xg[1][:, sh:S, 3], plane[1, 3].indirect(offs_t[:, sh // 16 : S // 16]))
         codes1 = keep.tile([P, S], U32, name="x_codes1", tag="w1_raw0_0", align_bytes=256)
-        for c0, c1 in ((0, S), (0, sh), (sh, S)):
+        for c0, c1 in ((0, S), (0, sh), (sh, S)) + parts:
             x_codes[1, c0, c1] = codes1[:, c0:c1]
         for s, c0 in enumerate((0, sh)):
             quantize_w1(0, s)
             quantize_x(1, c0, c0 + sh)
 
         h = [keep.tile([P, S], F32, name=f"h{t}", align_bytes=256) for t in range(TILES)]
-        h_banks = [["hA", "hB"], ["hC"], ["hD"], ["hA"]]
+        h_banks = [["hA", "hB", "z2", "z3"], ["hC"], ["hD"], ["hA"]]
 
         def first_layer(t):
-            w = S // len(h_banks[t])
-            accs = [psum.tile([P, w], F32, name=f"h_acc{t}_{b}", tag=b) for b in h_banks[t]]
+            cols = parts if t == 0 else ((0, S),)
+            accs = [psum.tile([P, c1 - c0], F32, name=f"h_acc{t}_{b}", tag=b) for b, (c0, c1) in zip(h_banks[t], cols)]
             for s in range(PASSES):
-                for i, acc in enumerate(accs):
+                for acc, (c0, c1) in zip(accs, cols):
                     nc.tensor.matmul_mx(
                         out=acc[:],
                         lhsT=w1_codes[t][:, s * P : (s + 1) * P].bitcast(FP8X4),
                         lhsT_scale=w1_scales[t][:, s * P : (s + 1) * P],
-                        rhs=x_codes[s, i * w, (i + 1) * w].bitcast(FP8X4),
-                        rhs_scale=x_scales[s][:, i * w : (i + 1) * w],
+                        rhs=x_codes[s, c0, c1].bitcast(FP8X4),
+                        rhs_scale=x_scales[s][:, c0:c1],
                         start=(s == 0),
                         stop=(s == PASSES - 1),
                     )
-            for i, acc in enumerate(accs):
-                if i == 0 or t > 0:
-                    nc.scalar.activation(h[t][:, i * w : (i + 1) * w], acc[:], RELU)
+            for acc, (c0, c1) in zip(accs, cols):
+                if t > 0:
+                    nc.scalar.activation(h[t][:, c0:c1], acc[:], RELU)
                 else:
-                    nc.vector.tensor_scalar_max(h[t][:, i * w : (i + 1) * w], acc[:], 0.0)
+                    nc.vector.tensor_scalar_max(h[t][:, c0:c1], acc[:], 0.0)
 
         def prepare(t):
             lay_w1(t, 0)
@@ -172,8 +173,11 @@ def tile_picked_sage_relu_e_kernel(tc, xT, w1, w2, gate, offs, pos1, pos2, pos3,
         def round_z(copy, t, c, acc):
             copy(zt[c][:, :, 32 * t : 32 * (t + 1), :], acc.rearrange("v (q a e) -> v a q e", a=2, e=2))
 
-        prepare(1)
+        lay_w1(1, 0)
+        lay_w1(1, 1)
+        quantize_w1(1, 0)
         first_layer(0)
+        quantize_w1(1, 1)
         first_layer(1)
         prepare(2)
         prepare(3)

@@ -31,7 +31,7 @@ def tile_picked_sage_relu_e_kernel(tc, xT, w1, w2, gate, offs, pos1, pos2, pos3,
 
         x_rows = xT.rearrange("(s p j) t -> s p j t", p=P, j=PACK)
         w1_rows = w1.rearrange("(s p j) c -> s p j c", p=P, j=PACK)
-        pieces = [[(0, 2), (2, 2)], [(0, 1), (1, 1), (2, 1), (3, 1)]]
+        pieces = [[(0, 2), (2, 1), (3, 1)], [(0, 1), (1, 1), (2, 1), (3, 1)]]
         w1_raw = {(t, s): keep.tile([P, PACK, P], F32, name=f"w1_raw{t}_{s}", align_bytes=256) for t in range(TILES) for s in range(PASSES)}
         w2_raw = keep.tile([P, PACK, N], F32, name="w2_raw", align_bytes=256)
         gates = [keep.tile([P, V], F32, name=f"gates{d}", align_bytes=256) for d in range(D)]
@@ -66,7 +66,8 @@ def tile_picked_sage_relu_e_kernel(tc, xT, w1, w2, gate, offs, pos1, pos2, pos3,
         x_codes = {}
         x_scales = [keep.tile([P, S], U8, name=f"x_scales{s}", align_bytes=256) for s in range(PASSES)]
         w1g = {(t, s): keep.tile([P, P * PACK], BF16, name=f"w1g{t}_{s}", align_bytes=256) for t in range(TILES) for s in range(PASSES)}
-        w1_codes = [keep.tile([P, PASSES * P], U32, name=f"w1_codes{t}", align_bytes=256) for t in range(TILES)]
+        w1_codes = {}
+        codes_in = {(1, 1): "w1_codes0_1", (2, 0): "w1g1_1"}
         w1_scales = [keep.tile([P, PASSES * P], U8, name=f"w1_scales{t}", align_bytes=256) for t in range(TILES)]
 
         def quantize(codes, scales, grouped):
@@ -76,7 +77,8 @@ def tile_picked_sage_relu_e_kernel(tc, xT, w1, w2, gate, offs, pos1, pos2, pos3,
             quantize(x_codes[s, c0, c1], x_scales[s][:, c0:c1], xg[s][:, c0:c1, :].rearrange("p n j -> p (n j)"))
 
         def quantize_w1(t, s):
-            quantize(w1_codes[t][:, s * P : (s + 1) * P], w1_scales[t][:, s * P : (s + 1) * P], w1g[t, s][:])
+            w1_codes[t, s] = keep.tile([P, P], U32, name=f"w1_codes{t}_{s}", tag=codes_in.get((t, s), f"w1_codes{t}_{s}"), align_bytes=256)
+            quantize(w1_codes[t, s][:], w1_scales[t][:, s * P : (s + 1) * P], w1g[t, s][:])
 
         def interleave(dst, src):
             return dst.rearrange("p (c i) j -> p c j i", i=4), src.rearrange("p j (c i) -> p c j i", i=4)
@@ -119,9 +121,11 @@ def tile_picked_sage_relu_e_kernel(tc, xT, w1, w2, gate, offs, pos1, pos2, pos3,
         codes1 = keep.tile([P, S], U32, name="x_codes1", tag="w1_raw0_0", align_bytes=256)
         for c0, c1 in ((0, S), (0, sh), (sh, S)) + parts:
             x_codes[1, c0, c1] = codes1[:, c0:c1]
-        for s, c0 in enumerate((0, sh)):
-            quantize_w1(0, s)
-            quantize_x(1, c0, c0 + sh)
+        quantize_w1(0, 0)
+        quantize_x(1, 0, sh)
+        quantize_x(1, *parts[2])
+        quantize_w1(0, 1)
+        quantize_x(1, *parts[3])
 
         h = [keep.tile([P, S], F32, name=f"h{t}", align_bytes=256) for t in range(TILES)]
         h_banks = [["hA", "hB", "z2", "z3"], ["hC"], ["hD"], ["hA"]]
@@ -133,7 +137,7 @@ def tile_picked_sage_relu_e_kernel(tc, xT, w1, w2, gate, offs, pos1, pos2, pos3,
                 for acc, (c0, c1) in zip(accs, cols):
                     nc.tensor.matmul_mx(
                         out=acc[:],
-                        lhsT=w1_codes[t][:, s * P : (s + 1) * P].bitcast(FP8X4),
+                        lhsT=w1_codes[t, s][:].bitcast(FP8X4),
                         lhsT_scale=w1_scales[t][:, s * P : (s + 1) * P],
                         rhs=x_codes[s, c0, c1].bitcast(FP8X4),
                         rhs_scale=x_scales[s][:, c0:c1],

@@ -88,13 +88,11 @@ def tile_picked_sage_relu_e_kernel(tc, xT, w1, w2, gate, offs, pos1, pos2, pos3,
             copy = nc.vector.tensor_copy if (t, s) == (1, 1) else nc.scalar.copy
             copy(*interleave(dst, w1_raw[t, s][:]))
 
-        picked = [
-            keep.tile([P, PACK, S], F32, name="picked0", align_bytes=256),
-            keep.tile([P, 2, S], F32, name="picked1", align_bytes=256),
-        ]
+        picked = [keep.tile([P, PACK, S], F32, name="picked0", align_bytes=256)]
         for j in range(PACK):
             nc.vector.tensor_copy(picked[0][:, j, :], plane[0, j].indirect(offs_t[:]))
-        nc.scalar.copy(*interleave(xg[0][:], picked[0][:]))
+        nc.scalar.copy(*interleave(xg[0][:, 0:sh, :], picked[0][:, :, 0:sh]))
+        nc.vector.tensor_copy(*interleave(xg[0][:, sh:S, :], picked[0][:, :, sh:S]))
         turned = psum.tile([P, halves, P], F32, name="gate_turned", tag="hA")
         for c in range(halves):
             nc.tensor.transpose(turned[:, c, :], gate_rows[:, c * P : (c + 1) * P], ident[:])
@@ -105,14 +103,13 @@ def tile_picked_sage_relu_e_kernel(tc, xT, w1, w2, gate, offs, pos1, pos2, pos3,
             for c in range(halves):
                 nc.tensor.transpose(spread[:, c, :], gate_cols[:, c, d : d + 1].to_broadcast([P, P]), ident[:])
             nc.scalar.copy(gates[d][:], spread[:].rearrange("p c v -> p (c v)"))
-        nc.vector.tensor_copy(picked[1][:, 0, :], plane[1, 0].indirect(offs_t[:]))
-        codes0 = keep.tile([P, S], U32, name="x_codes0", align_bytes=256)
+        nc.vector.tensor_copy(xg[1][:, :, 0], plane[1, 0].indirect(offs_t[:]))
+        codes0 = keep.tile([P, S], U32, name="x_codes0", tag="x1_0", align_bytes=256)
         parts = tuple((c, c + P) for c in range(0, S, P))
         for c0, c1 in ((0, S),) + parts:
             x_codes[0, c0, c1] = codes0[:, c0:c1]
         quantize_x(0, 0, S)
-        nc.vector.tensor_copy(picked[1][:, 1, :], plane[1, 1].indirect(offs_t[:]))
-        nc.scalar.copy(*interleave(xg[1][:, :, 0:2], picked[1][:]))
+        nc.vector.tensor_copy(xg[1][:, :, 1], plane[1, 1].indirect(offs_t[:]))
         nc.vector.tensor_copy(xg[1][:, :, 2], plane[1, 2].indirect(offs_t[:]))
         lay_w1(0, 0)
         lay_w1(0, 1)

@@ -8,6 +8,10 @@ P = 128
 PACK = 4
 PASSES = K // (P * PACK)
 TILES = H // P
+HALVES = V // P
+LIST_ROWS = 16
+LINE = 4
+GRID = 256
 FLOPS = 2 * K * S * H + 2 * H * V * N
 
 F32 = mybir.dt.float32
@@ -26,28 +30,27 @@ def tile_picked_sage_relu_e_kernel(tc, xT, w1, w2, gate, offs, pos1, pos2, pos3,
         keep = ctx.enter_context(tc.tile_pool(name="keep", bufs=1))
         psum = ctx.enter_context(tc.psum_pool(name="psum", bufs=1))
 
-        offs_t = keep.tile([P, S // 16], U16, name="offs_t")
-        pos_t = [keep.tile([P, V // 16], U16, name=f"pos_t{d}") for d in range(D)]
+        offs_t = keep.tile([P, S // LIST_ROWS], U16, name="offs_t")
+        pos_t = [keep.tile([P, V // LIST_ROWS], U16, name=f"pos_t{d}") for d in range(D)]
 
         x_rows = xT.rearrange("(s p j) t -> s p j t", p=P, j=PACK)
         w1_rows = w1.rearrange("(s p j) c -> s p j c", p=P, j=PACK)
-        pieces = [[(0, 2), (2, 1), (3, 1)], [(0, 1), (1, 1), (2, 1), (3, 1)]]
-        w1_raw = {(t, s): keep.tile([P, PACK, P], F32, name=f"w1_raw{t}_{s}", align_bytes=256) for t in range(TILES) for s in range(PASSES)}
-        w2_raw = keep.tile([P, PACK, N], F32, name="w2_raw", align_bytes=256)
-        gates = [keep.tile([P, V], F32, name=f"gates{d}", align_bytes=256) for d in range(D)]
+        x_loads = [[(0, 2), (2, 1), (3, 1)], [(j, 1) for j in range(PACK)]]
+        w1_raw = {(t, s): keep.tile([P, PACK, P], F32, name=f"w1_raw{t}_{s}", align_bytes=GRID) for t in range(TILES) for s in range(PASSES)}
+        w2_raw = keep.tile([P, PACK, N], F32, name="w2_raw", align_bytes=GRID)
+        gates = [keep.tile([P, V], F32, name=f"gates{d}", align_bytes=GRID) for d in range(D)]
         plane = {}
-
         for s in range(PASSES):
-            for j0, n in pieces[s]:
-                x_t = keep.tile([P, n, T], F32, name=f"x{s}_{j0}", align_bytes=256)
+            for j0, n in x_loads[s]:
+                x_t = keep.tile([P, n, T], F32, name=f"x{s}_{j0}", align_bytes=GRID)
                 nc.sync.dma_start(x_t[:], x_rows[s][:, j0 : j0 + n, :])
                 if (s, j0) == (0, 0):
                     nc.sync.dma_start(offs_t[:], offs)
                 for j in range(n):
                     plane[s, j0 + j] = x_t[:, j, :]
             if s == 0:
-                for d, p in enumerate((pos1, pos2, pos3)):
-                    nc.sync.dma_start(pos_t[d][:], p)
+                for d, pos in enumerate((pos1, pos2, pos3)):
+                    nc.sync.dma_start(pos_t[d][:], pos)
         for t in range(TILES):
             for s in range(PASSES):
                 nc.sync.dma_start(w1_raw[t, s][:], w1_rows[s][:, :, t * P : (t + 1) * P])
@@ -56,171 +59,175 @@ def tile_picked_sage_relu_e_kernel(tc, xT, w1, w2, gate, offs, pos1, pos2, pos3,
         ident = keep.tile([P, P], F32, name="ident")
         make_identity(nc, ident[:])
 
-        halves = V // P
         gate_rows = keep.tile([P, V], F32, name="gate_rows")
         nc.gpsimd.memset(gate_rows[:], 0.0)
         nc.scalar.dma_start(gate_rows[0:D, :], gate[:, 0, :])
 
-        xg = [keep.tile([P, S, PACK], BF16, name=f"xg{s}", align_bytes=256) for s in range(PASSES)]
-        sh = S // 2
-        x_codes = {}
-        x_scales = [keep.tile([P, S], U8, name=f"x_scales{s}", align_bytes=256) for s in range(PASSES)]
-        w1g = {(t, s): keep.tile([P, P * PACK], BF16, name=f"w1g{t}_{s}", align_bytes=256) for t in range(TILES) for s in range(PASSES)}
+        x_grouped = [keep.tile([P, S, PACK], BF16, name=f"xg{s}", align_bytes=GRID) for s in range(PASSES)]
+        x_codes = []
+        x_scales = [keep.tile([P, S], U8, name=f"x_scales{s}", align_bytes=GRID) for s in range(PASSES)]
+        w1_grouped = {(t, s): keep.tile([P, P * PACK], BF16, name=f"w1g{t}_{s}", align_bytes=GRID) for t in range(TILES) for s in range(PASSES)}
         w1_codes = {}
-        codes_in = {(1, 1): "w1_codes0_1", (2, 0): "w1g1_1"}
-        w1_scales = [keep.tile([P, PASSES * P], U8, name=f"w1_scales{t}", align_bytes=256) for t in range(TILES)]
+        w1_scales = [keep.tile([P, PASSES * P], U8, name=f"w1_scales{t}", align_bytes=GRID) for t in range(TILES)]
 
         def quantize(codes, scales, grouped):
             nc.vector.quantize_mx(out=codes.bitcast(FP8X4), scales=scales, in_=grouped)
 
         def quantize_x(s, c0, c1):
-            quantize(x_codes[s, c0, c1], x_scales[s][:, c0:c1], xg[s][:, c0:c1, :].rearrange("p n j -> p (n j)"))
+            quantize(x_codes[s][:, c0:c1], x_scales[s][:, c0:c1], x_grouped[s][:, c0:c1, :].rearrange("p n j -> p (n j)"))
 
-        def quantize_w1(t, s):
-            w1_codes[t, s] = keep.tile([P, P], U32, name=f"w1_codes{t}_{s}", tag=codes_in.get((t, s), f"w1_codes{t}_{s}"), align_bytes=256)
-            quantize(w1_codes[t, s][:], w1_scales[t][:, s * P : (s + 1) * P], w1g[t, s][:])
+        def quantize_w1(t, s, buffer=None):
+            name = f"w1_codes{t}_{s}"
+            w1_codes[t, s] = keep.tile([P, P], U32, name=name, tag=buffer or name, align_bytes=GRID)
+            quantize(w1_codes[t, s][:], w1_scales[t][:, s * P : (s + 1) * P], w1_grouped[t, s][:])
 
         def interleave(dst, src):
-            return dst.rearrange("p (c i) j -> p c j i", i=4), src.rearrange("p j (c i) -> p c j i", i=4)
+            return dst.rearrange("p (c i) j -> p c j i", i=LINE), src.rearrange("p j (c i) -> p c j i", i=LINE)
 
-        def lay_w1(t, s):
-            dst = w1g[t, s][:].rearrange("p (m j) -> p m j", j=PACK)
-            copy = nc.vector.tensor_copy if (t, s) == (1, 1) else nc.scalar.copy
-            copy(*interleave(dst, w1_raw[t, s][:]))
+        def round_w1(copy, t, s):
+            copy(*interleave(w1_grouped[t, s][:].rearrange("p (m j) -> p m j", j=PACK), w1_raw[t, s][:]))
 
-        picked = [keep.tile([P, PACK, S], F32, name="picked0", align_bytes=256)]
+        half = S // 2
+        picked = keep.tile([P, PACK, S], F32, name="picked", align_bytes=GRID)
         for j in range(PACK):
-            nc.vector.tensor_copy(picked[0][:, j, :], plane[0, j].indirect(offs_t[:]))
-        nc.scalar.copy(*interleave(xg[0][:, 0:sh, :], picked[0][:, :, 0:sh]))
-        nc.vector.tensor_copy(*interleave(xg[0][:, sh:S, :], picked[0][:, :, sh:S]))
-        turned = psum.tile([P, halves, P], F32, name="gate_turned", tag="hA")
-        for c in range(halves):
+            nc.vector.tensor_copy(picked[:, j, :], plane[0, j].indirect(offs_t[:]))
+        nc.scalar.copy(*interleave(x_grouped[0][:, 0:half, :], picked[:, :, 0:half]))
+        nc.vector.tensor_copy(*interleave(x_grouped[0][:, half:S, :], picked[:, :, half:S]))
+
+        turned = psum.tile([P, HALVES, P], F32, name="gate_turned", tag="hA")
+        for c in range(HALVES):
             nc.tensor.transpose(turned[:, c, :], gate_rows[:, c * P : (c + 1) * P], ident[:])
-        gate_cols = keep.tile([P, halves, D], F32, name="gate_cols", tag="picked0", align_bytes=256)
+        gate_cols = keep.tile([P, HALVES, D], F32, name="gate_cols", tag="picked", align_bytes=GRID)
         nc.scalar.copy(gate_cols[:], turned[:, :, 0:D])
         for d, bank in enumerate(("hB", "hC", "hD")):
-            spread = psum.tile([P, halves, P], F32, name=f"gate_spread{d}", tag=bank)
-            for c in range(halves):
+            spread = psum.tile([P, HALVES, P], F32, name=f"gate_spread{d}", tag=bank)
+            for c in range(HALVES):
                 nc.tensor.transpose(spread[:, c, :], gate_cols[:, c, d : d + 1].to_broadcast([P, P]), ident[:])
             nc.scalar.copy(gates[d][:], spread[:].rearrange("p c v -> p (c v)"))
-        nc.vector.tensor_copy(xg[1][:, :, 0], plane[1, 0].indirect(offs_t[:]))
-        codes0 = keep.tile([P, S], U32, name="x_codes0", tag="x1_0", align_bytes=256)
-        parts = tuple((c, c + P) for c in range(0, S, P))
-        for c0, c1 in ((0, S),) + parts:
-            x_codes[0, c0, c1] = codes0[:, c0:c1]
+
+        nc.vector.tensor_copy(x_grouped[1][:, :, 0], plane[1, 0].indirect(offs_t[:]))
+        x_codes.append(keep.tile([P, S], U32, name="x_codes0", tag="x1_0", align_bytes=GRID))
         quantize_x(0, 0, S)
-        nc.vector.tensor_copy(xg[1][:, :, 1], plane[1, 1].indirect(offs_t[:]))
-        nc.vector.tensor_copy(xg[1][:, :, 2], plane[1, 2].indirect(offs_t[:]))
-        lay_w1(0, 0)
-        lay_w1(0, 1)
-        nc.vector.tensor_copy(xg[1][:, 0:sh, 3], plane[1, 3].indirect(offs_t[:, 0 : sh // 16]))
-        nc.vector.tensor_copy(xg[1][:, sh:S, 3], plane[1, 3].indirect(offs_t[:, sh // 16 : S // 16]))
-        codes1 = keep.tile([P, S], U32, name="x_codes1", tag="w1_raw0_0", align_bytes=256)
-        for c0, c1 in ((0, S), (0, sh), (sh, S)) + parts:
-            x_codes[1, c0, c1] = codes1[:, c0:c1]
+        for j in (1, 2):
+            nc.vector.tensor_copy(x_grouped[1][:, :, j], plane[1, j].indirect(offs_t[:]))
+        for s in range(PASSES):
+            round_w1(nc.scalar.copy, 0, s)
+        for c0 in (0, half):
+            nc.vector.tensor_copy(x_grouped[1][:, c0 : c0 + half, 3], plane[1, 3].indirect(offs_t[:, c0 // LIST_ROWS : (c0 + half) // LIST_ROWS]))
+        x_codes.append(keep.tile([P, S], U32, name="x_codes1", tag="w1_raw0_0", align_bytes=GRID))
         quantize_w1(0, 0)
-        quantize_x(1, 0, sh)
-        quantize_x(1, *parts[2])
+        quantize_x(1, 0, half)
+        quantize_x(1, half, S - P)
         quantize_w1(0, 1)
-        quantize_x(1, *parts[3])
+        quantize_x(1, S - P, S)
 
-        h = [keep.tile([P, S], F32, name=f"h{t}", align_bytes=256) for t in range(TILES)]
-        h_banks = [["hA", "hB", "z2", "z3"], ["hC"], ["hD"], ["hA"]]
+        h = [keep.tile([P, S], F32, name=f"h{t}", align_bytes=GRID) for t in range(TILES)]
 
-        def first_layer(t):
-            cols = parts if t == 0 else ((0, S),)
-            accs = [psum.tile([P, c1 - c0], F32, name=f"h_acc{t}_{b}", tag=b) for b, (c0, c1) in zip(h_banks[t], cols)]
+        def first_layer(t, banks):
+            width = S // len(banks)
+            accs = [psum.tile([P, width], F32, name=f"h_acc{t}_{bank}", tag=bank) for bank in banks]
             for s in range(PASSES):
-                for acc, (c0, c1) in zip(accs, cols):
+                for i, acc in enumerate(accs):
                     nc.tensor.matmul_mx(
                         out=acc[:],
                         lhsT=w1_codes[t, s][:].bitcast(FP8X4),
                         lhsT_scale=w1_scales[t][:, s * P : (s + 1) * P],
-                        rhs=x_codes[s, c0, c1].bitcast(FP8X4),
-                        rhs_scale=x_scales[s][:, c0:c1],
+                        rhs=x_codes[s][:, i * width : (i + 1) * width].bitcast(FP8X4),
+                        rhs_scale=x_scales[s][:, i * width : (i + 1) * width],
                         start=(s == 0),
                         stop=(s == PASSES - 1),
                     )
-            for acc, (c0, c1) in zip(accs, cols):
-                if t > 0:
-                    nc.scalar.activation(h[t][:, c0:c1], acc[:], RELU)
+            for i, acc in enumerate(accs):
+                if t == 0:
+                    nc.vector.tensor_scalar_max(h[t][:, i * width : (i + 1) * width], acc[:], 0.0)
                 else:
-                    nc.vector.tensor_scalar_max(h[t][:, c0:c1], acc[:], 0.0)
+                    nc.scalar.activation(h[t][:, i * width : (i + 1) * width], acc[:], RELU)
 
-        def prepare(t):
-            lay_w1(t, 0)
-            lay_w1(t, 1)
-            quantize_w1(t, 0)
+        w2_grouped = keep.tile([P, N, PACK], BF16, name="w2g", align_bytes=GRID)
+        w2_scales = keep.tile([P, N], U8, name="w2_scales", align_bytes=GRID)
+
+        round_w1(nc.scalar.copy, 1, 0)
+        round_w1(nc.vector.tensor_copy, 1, 1)
+        quantize_w1(1, 0)
+        first_layer(0, ("hA", "hB", "z2", "z3"))
+        quantize_w1(1, 1, "w1_codes0_1")
+        first_layer(1, ("hC",))
+        for t in (2, 3):
+            for s in range(PASSES):
+                round_w1(nc.scalar.copy, t, s)
+            quantize_w1(t, 0, "w1g1_1" if t == 2 else None)
             quantize_w1(t, 1)
+        first_layer(2, ("hD",))
+        first_layer(3, ("hA",))
+        nc.scalar.copy(*interleave(w2_grouped[:], w2_raw[:]))
 
-        u = {}
-        reuse = {(0, 0): (1, "u0"), (0, 1): (1, "w1_raw2_0"), (0, 2): (2, "w1_raw2_1"), (1, 1): (1, "w1_raw3_0"), (1, 2): (1, "w1_raw3_1"), (2, 0): (6, "u2")}
-        zt = []
-        w2g = keep.tile([P, N, PACK], BF16, name="w2g", align_bytes=256)
-        w2_scales = keep.tile([P, N], U8, name="w2_scales", align_bytes=256)
+        z_turned = [keep.tile([P, 2, P, 2], BF16, name=f"zt{c}", tag=buffer, align_bytes=GRID) for c, buffer in enumerate(("w2_raw", "w1g3_1"))]
+        term = {}
+
+        def make_terms(t, d, n, buffer):
+            terms = keep.tile([P, n, V], F32, name=f"u{t}_{d}", tag=buffer, align_bytes=GRID)
+            for i in range(n):
+                term[divmod(D * t + d + i, D)] = terms[:, i, :]
 
         def fetch(t, d, v0, v1):
-            if v0 == 0 and (t, d) in reuse:
-                n, tag = reuse[t, d]
-                terms = keep.tile([P, n, V], F32, name=f"u{t}_{d}", tag=tag, align_bytes=256)
-                for i in range(n):
-                    u[divmod(D * t + d + i, D)] = terms[:, i, :]
-            nc.vector.tensor_tensor(u[t, d][:, v0:v1], h[t][:].indirect(pos_t[d][:, v0 // 16 : v1 // 16]), gates[d][:, v0:v1], MULT)
+            offsets = pos_t[d][:, v0 // LIST_ROWS : v1 // LIST_ROWS]
+            nc.vector.tensor_tensor(term[t, d][:, v0:v1], h[t][:].indirect(offsets), gates[d][:, v0:v1], MULT)
 
         def turn_and_add(t, c, acc, turns):
             for i, d in enumerate(turns):
-                nc.tensor.matmul(acc, u[t, d][:, c * P : (c + 1) * P], ident[:], start=(i == 0), stop=(i == D - 1), is_transpose=True)
+                nc.tensor.matmul(acc, term[t, d][:, c * P : (c + 1) * P], ident[:], start=(i == 0), stop=(i == D - 1), is_transpose=True)
 
-        def round_z(copy, t, c, acc):
-            copy(zt[c][:, :, 32 * t : 32 * (t + 1), :], acc.rearrange("v (q a e) -> v a q e", a=2, e=2))
+        def z_views(t, c, acc):
+            q = P // PACK
+            return z_turned[c][:, :, q * t : q * (t + 1), :], acc.rearrange("v (q a e) -> v a q e", a=2, e=2)
 
-        lay_w1(1, 0)
-        lay_w1(1, 1)
-        quantize_w1(1, 0)
-        first_layer(0)
-        quantize_w1(1, 1)
-        first_layer(1)
-        prepare(2)
-        prepare(3)
-        first_layer(2)
-        first_layer(3)
-        nc.scalar.copy(*interleave(w2g[:], w2_raw[:]))
-        for c, tag in enumerate(("w2_raw", "w1g3_1")):
-            zt.append(keep.tile([P, 2, P, 2], BF16, name=f"zt{c}", tag=tag, align_bytes=256))
-        last = TILES - 1
-        for t in range(last - 1):
+        for t in range(2):
             for d in range(D):
+                if t == 0 and d == 0:
+                    make_terms(t, d, 1, "u0")
+                elif d > 0:
+                    with_next_tile = 1 if (t, d) == (0, D - 1) else 0
+                    make_terms(t, d, 1 + with_next_tile, f"w1_raw{t + 2}_{d - 1}")
                 fetch(t, d, 0, V)
-            acc = psum.tile([P, halves, P], F32, name=f"z_acc{t}", tag=f"z{t % 2}")
-            for c in range(halves):
-                turn_and_add(t, c, acc[:, c, :], (2, 1, 0))
-            for c in range(halves):
-                round_z(nc.scalar.copy, t, c, acc[:, c, :])
-        accs = [psum.tile([P, P], F32, name=f"z_acc{last - 1}_{c}", tag=("hB", "hC")[c]) for c in range(halves)]
+            acc = psum.tile([P, HALVES, P], F32, name=f"z_acc{t}", tag=f"z{t}")
+            for c in range(HALVES):
+                turn_and_add(t, c, acc[:, c, :], reversed(range(D)))
+            for c in range(HALVES):
+                nc.scalar.copy(*z_views(t, c, acc[:, c, :]))
+
+        accs = [psum.tile([P, P], F32, name=f"z_acc2_{c}", tag=bank) for c, bank in enumerate(("hB", "hC"))]
+        make_terms(2, 0, 2 * D, "u2")
         for d in range(D):
-            fetch(last - 1, d, 0, V)
-        for c in range(halves):
-            turn_and_add(last - 1, c, accs[c][:], (0, 1, 2))
-            round_z(nc.scalar.copy, last - 1, c, accs[c][:])
-        accs = [psum.tile([P, P], F32, name=f"z_acc{last}_{c}", tag=f"z{2 + c}") for c in range(halves)]
-        for c in range(halves):
+            fetch(2, d, 0, V)
+        for c in range(HALVES):
+            turn_and_add(2, c, accs[c][:], range(D))
+            nc.scalar.copy(*z_views(2, c, accs[c][:]))
+        accs = [psum.tile([P, P], F32, name=f"z_acc3_{c}", tag=bank) for c, bank in enumerate(("z2", "z3"))]
+        for c in range(HALVES):
             for d in range(D):
-                fetch(last, d, c * P, (c + 1) * P)
-            turn_and_add(last, c, accs[c][:], (0, 1, 2))
-        w2_codes = keep.tile([P, N], U32, name="w2_codes", tag=f"gates{D - 1}", align_bytes=256)
-        quantize(w2_codes[:], w2_scales[:], w2g[:].rearrange("p m j -> p (m j)"))
-        for c in range(halves):
+                fetch(3, d, c * P, (c + 1) * P)
+            turn_and_add(3, c, accs[c][:], range(D))
+
+        w2_codes = keep.tile([P, N], U32, name="w2_codes", tag=f"gates{D - 1}", align_bytes=GRID)
+        quantize(w2_codes[:], w2_scales[:], w2_grouped[:].rearrange("p m j -> p (m j)"))
+
+        for c in range(HALVES):
             copy = nc.scalar.copy if c == 0 else nc.vector.tensor_copy
-            round_z(copy, last, c, accs[c][:])
+            dst, src = z_views(3, c, accs[c][:])
+            if c == 0:
+                copy(dst, src)
+            else:
+                for a in range(2):
+                    copy(dst[:, a], src[:, a])
             back = psum.tile([P, 2, P], F32, name=f"back{c}", tag=("hD", "z0")[c])
-            words = zt[c][:].rearrange("v a p e -> v (a p e)").bitcast(F32)
+            pairs = z_turned[c][:].rearrange("v a p e -> v (a p e)").bitcast(F32)
             for a in range(2):
-                nc.tensor.transpose(back[:, a, :], words[:, a * P : (a + 1) * P], ident[:])
-            zg = keep.tile([P, P * PACK], BF16, name=f"zg{c}", align_bytes=256)
-            copy(zg[:].bitcast(F32).rearrange("p (v a) -> p v a", a=2), back[:].rearrange("p a v -> p v a"))
-            z_codes = keep.tile([P, P], U32, name=f"z_codes{c}", align_bytes=256)
-            z_scales = keep.tile([P, P], U8, name=f"z_scales{c}", align_bytes=256)
-            quantize(z_codes[:], z_scales[:], zg[:])
+                nc.tensor.transpose(back[:, a, :], pairs[:, a * P : (a + 1) * P], ident[:])
+            z_grouped = keep.tile([P, P * PACK], BF16, name=f"zg{c}", align_bytes=GRID)
+            copy(z_grouped[:].bitcast(F32).rearrange("p (v a) -> p v a", a=2), back[:].rearrange("p a v -> p v a"))
+            z_codes = keep.tile([P, P], U32, name=f"z_codes{c}", align_bytes=GRID)
+            z_scales = keep.tile([P, P], U8, name=f"z_scales{c}", align_bytes=GRID)
+            quantize(z_codes[:], z_scales[:], z_grouped[:])
             o_acc = psum.tile([P, P], F32, name=f"o_acc{c}", tag=("hA", "z1")[c])
             nc.tensor.matmul_mx(
                 out=o_acc[:],
@@ -231,6 +238,6 @@ def tile_picked_sage_relu_e_kernel(tc, xT, w1, w2, gate, offs, pos1, pos2, pos3,
                 start=True,
                 stop=True,
             )
-            res = keep.tile([P, P], F32, name=f"res{c}", align_bytes=256)
+            res = keep.tile([P, P], F32, name=f"res{c}", align_bytes=GRID)
             copy(res[:], o_acc[:])
             nc.sync.dma_start(out[:, c * P : (c + 1) * P], res[:])

@@ -66,7 +66,7 @@ def tile_picked_sage_relu_e_kernel(tc, xT, w1, w2, gate, offs, pos1, pos2, pos3,
         x_grouped = [keep.tile([P, S, PACK], BF16, name=f"xg{s}", align_bytes=GRID) for s in range(PASSES)]
         x_codes = []
         x_scales = [keep.tile([P, S], U8, name=f"x_scales{s}", align_bytes=GRID) for s in range(PASSES)]
-        w1_grouped = {(t, s): keep.tile([P, P * PACK], BF16, name=f"w1g{t}_{s}", align_bytes=GRID) for t in range(TILES) for s in range(PASSES)}
+        w1_grouped = {(t, s): keep.tile([P, P * PACK], BF16, name=f"w1g{t}_{s}", align_bytes=GRID) for t in range(TILES) for s in range(PASSES) if (t, s) != (3, 0)}
         w1_codes = {}
         w1_scales = [keep.tile([P, PASSES * P], U8, name=f"w1_scales{t}", align_bytes=GRID) for t in range(TILES)]
 
@@ -152,6 +152,7 @@ def tile_picked_sage_relu_e_kernel(tc, xT, w1, w2, gate, offs, pos1, pos2, pos3,
         first_layer(0, ("hA", "hB", "z2", "z3"))
         quantize_w1(1, 1, "w1_codes0_1")
         first_layer(1, ("hC",))
+        w1_grouped[3, 0] = keep.tile([P, P * PACK], BF16, name="w1g3_0", tag="w1_codes0_1", align_bytes=GRID)
         for t in (2, 3):
             for s in range(PASSES):
                 round_w1(nc.scalar.copy, t, s)

@@ -11,6 +11,8 @@ TILES = H // P
 HALVES = V // P
 LIST_ROWS = 16
 LINE = 4
+RUN = 8
+KIB = 1024
 GRID = 256
 FLOPS = 2 * K * S * H + 2 * H * V * N
 
@@ -28,6 +30,7 @@ def tile_picked_sage_relu_e_kernel(tc, xT, w1, w2, gate, offs, pos1, pos2, pos3,
     nc = tc.nc
     with ExitStack() as ctx:
         keep = ctx.enter_context(tc.tile_pool(name="keep", bufs=1))
+        late = ctx.enter_context(tc.tile_pool(name="late", bufs=1))
         psum = ctx.enter_context(tc.psum_pool(name="psum", bufs=1))
 
         offs_t = keep.tile([P, S // LIST_ROWS], U16, name="offs_t")
@@ -36,7 +39,9 @@ def tile_picked_sage_relu_e_kernel(tc, xT, w1, w2, gate, offs, pos1, pos2, pos3,
         x_rows = xT.rearrange("(s p j) t -> s p j t", p=P, j=PACK)
         w1_rows = w1.rearrange("(s p j) c -> s p j c", p=P, j=PACK)
         x_loads = [[(0, 2), (2, 1), (3, 1)], [(j, 1) for j in range(PACK)]]
-        w1_raw = {(t, s): keep.tile([P, PACK, P], F32, name=f"w1_raw{t}_{s}", align_bytes=GRID) for t in range(TILES) for s in range(PASSES)}
+        w1_raw = {(t, s): keep.tile([P, PACK, P], F32, name=f"w1_raw{t}_{s}", align_bytes=GRID) for t in range(TILES) for s in range(PASSES) if t < 2 or s == 0}
+        for t in (2, 3):
+            w1_raw[t, 1] = late.tile([P, PACK, P], F32, name=f"w1_raw{t}_1", offset=(4 * (t - 2) + 1) * KIB, align_bytes=GRID)
         w2_raw = keep.tile([P, PACK, N], F32, name="w2_raw", align_bytes=GRID)
         gates = [keep.tile([P, V], F32, name=f"gates{d}", align_bytes=GRID) for d in range(D)]
         plane = {}
@@ -48,20 +53,30 @@ def tile_picked_sage_relu_e_kernel(tc, xT, w1, w2, gate, offs, pos1, pos2, pos3,
                     nc.sync.dma_start(offs_t[:], offs)
                 for j in range(n):
                     plane[s, j0 + j] = x_t[:, j, :]
-            if s == 0:
-                for d, pos in enumerate((pos1, pos2, pos3)):
-                    nc.sync.dma_start(pos_t[d][:], pos)
         for t in range(TILES):
             for s in range(PASSES):
                 nc.sync.dma_start(w1_raw[t, s][:], w1_rows[s][:, :, t * P : (t + 1) * P])
+                d = PASSES * t + s - 3
+                if 0 <= d < D:
+                    nc.sync.dma_start(pos_t[d][:], (pos1, pos2, pos3)[d])
         nc.sync.dma_start(w2_raw[:], w2.rearrange("(p j) m -> p j m", j=PACK))
 
         ident = keep.tile([P, P], F32, name="ident")
         make_identity(nc, ident[:])
 
-        gate_rows = keep.tile([P, V], F32, name="gate_rows")
-        nc.gpsimd.memset(gate_rows[:], 0.0)
-        nc.scalar.dma_start(gate_rows[0:D, :], gate[:, 0, :])
+        gate_cols = keep.tile([P, D, RUN], F32, name="gate_cols")
+        nc.scalar.dma_start(gate_cols[0 : V // RUN], gate[:, 0, :].rearrange("d (q i) -> q d i", i=RUN))
+        nc.gpsimd.memset(gate_cols[32:64], 0.0)
+        nc.gpsimd.memset(gate_cols[64:P], 0.0)
+
+        for d, banks in enumerate((("hA", "hB"), ("hC", "hD"), ("z0", "z1"))):
+            for b, bank in enumerate(banks):
+                spread = psum.tile([P, LINE, P], F32, name=f"gate_spread{d}_{b}", tag=bank)
+                for i in range(LINE):
+                    column = gate_cols[:, d, LINE * b + i : LINE * b + i + 1]
+                    nc.tensor.transpose(spread[:, i, :], column.to_broadcast([P, P]), ident[:])
+                dst = gates[d][:].rearrange("p (q i) -> p q i", i=RUN)[:, :, LINE * b : LINE * (b + 1)]
+                nc.scalar.copy(dst, spread[:, :, 0 : V // RUN].rearrange("p i q -> p q i"))
 
         x_grouped = [keep.tile([P, S, PACK], BF16, name=f"xg{s}", align_bytes=GRID) for s in range(PASSES)]
         x_codes = []
@@ -94,17 +109,6 @@ def tile_picked_sage_relu_e_kernel(tc, xT, w1, w2, gate, offs, pos1, pos2, pos3,
         nc.scalar.copy(*interleave(x_grouped[0][:, 0:half, :], picked[:, :, 0:half]))
         nc.vector.tensor_copy(*interleave(x_grouped[0][:, half:S, :], picked[:, :, half:S]))
 
-        turned = psum.tile([P, HALVES, P], F32, name="gate_turned", tag="hA")
-        for c in range(HALVES):
-            nc.tensor.transpose(turned[:, c, :], gate_rows[:, c * P : (c + 1) * P], ident[:])
-        gate_cols = keep.tile([P, HALVES, D], F32, name="gate_cols", tag="picked", align_bytes=GRID)
-        nc.scalar.copy(gate_cols[:], turned[:, :, 0:D])
-        for d, bank in enumerate(("hB", "hC", "hD")):
-            spread = psum.tile([P, HALVES, P], F32, name=f"gate_spread{d}", tag=bank)
-            for c in range(HALVES):
-                nc.tensor.transpose(spread[:, c, :], gate_cols[:, c, d : d + 1].to_broadcast([P, P]), ident[:])
-            nc.scalar.copy(gates[d][:], spread[:].rearrange("p c v -> p (c v)"))
-
         nc.vector.tensor_copy(x_grouped[1][:, :, 0], plane[1, 0].indirect(offs_t[:]))
         x_codes.append(keep.tile([P, S], U32, name="x_codes0", tag="x1_0", align_bytes=GRID))
         quantize_x(0, 0, S)
@@ -121,7 +125,7 @@ def tile_picked_sage_relu_e_kernel(tc, xT, w1, w2, gate, offs, pos1, pos2, pos3,
         quantize_w1(0, 1)
         quantize_x(1, S - P, S)
 
-        h = [keep.tile([P, S], F32, name=f"h{t}", align_bytes=GRID) for t in range(TILES)]
+        h = [keep.tile([P, S], F32, name=f"h{t}", align_bytes=GRID) if t not in (1, 2) else late.tile([P, S], F32, name=f"h{t}", offset=(4 * (t - 1) + 2) * KIB, align_bytes=GRID) for t in range(TILES)]
 
         def first_layer(t, banks):
             width = S // len(banks)
@@ -166,7 +170,10 @@ def tile_picked_sage_relu_e_kernel(tc, xT, w1, w2, gate, offs, pos1, pos2, pos3,
         term = {}
 
         def make_terms(t, d, n, buffer):
-            terms = keep.tile([P, n, V], F32, name=f"u{t}_{d}", tag=buffer, align_bytes=GRID)
+            if buffer in ("w1_raw2_1", "w1_raw3_1"):
+                terms = late.tile([P, n, V], F32, name=f"u{t}_{d}", offset=(4 * t + 2 - n) * KIB, align_bytes=GRID)
+            else:
+                terms = keep.tile([P, n, V], F32, name=f"u{t}_{d}", tag=buffer, align_bytes=GRID)
             for i in range(n):
                 term[divmod(D * t + d + i, D)] = terms[:, i, :]
 

@@ -232,20 +232,25 @@ def tile_picked_sage_relu_e_kernel(tc, xT, w1, w2, gate, offs, pos1, pos2, pos3,
             for a in range(2):
                 nc.tensor.transpose(back[:, a, :], pairs[:, a * P : (a + 1) * P], ident[:])
             z_grouped = keep.tile([P, P * PACK], BF16, name=f"zg{c}", align_bytes=GRID)
-            copy(z_grouped[:].bitcast(F32).rearrange("p (v a) -> p v a", a=2), back[:].rearrange("p a v -> p v a"))
             z_codes = keep.tile([P, P], U32, name=f"z_codes{c}", align_bytes=GRID)
             z_scales = keep.tile([P, P], U8, name=f"z_scales{c}", align_bytes=GRID)
-            quantize(z_codes[:], z_scales[:], z_grouped[:])
-            o_acc = psum.tile([P, P], F32, name=f"o_acc{c}", tag=("hA", "z1")[c])
-            nc.tensor.matmul_mx(
-                out=o_acc[:],
-                lhsT=w2_codes[:].bitcast(FP8X4),
-                lhsT_scale=w2_scales[:],
-                rhs=z_codes[:].bitcast(FP8X4),
-                rhs_scale=z_scales[:],
-                start=True,
-                stop=True,
-            )
             res = keep.tile([P, P], F32, name=f"res{c}", align_bytes=GRID)
-            copy(res[:], o_acc[:])
+            banks = (("hA",), ("z1", "hB"))[c]
+            step = P // len(banks)
+            for i, bank in enumerate(banks):
+                cols = slice(i * step, (i + 1) * step)
+                words = z_grouped[:, PACK * cols.start : PACK * cols.stop]
+                nc.scalar.copy(words.bitcast(F32).rearrange("p (v a) -> p v a", a=2), back[:, :, cols].rearrange("p a v -> p v a"))
+                quantize(z_codes[:, cols], z_scales[:, cols], words)
+                o_acc = psum.tile([P, step], F32, name=f"o_acc{bank}", tag=bank)
+                nc.tensor.matmul_mx(
+                    out=o_acc[:],
+                    lhsT=w2_codes[:].bitcast(FP8X4),
+                    lhsT_scale=w2_scales[:],
+                    rhs=z_codes[:, cols].bitcast(FP8X4),
+                    rhs_scale=z_scales[:, cols],
+                    start=True,
+                    stop=True,
+                )
+                copy(res[:, cols], o_acc[:])
             nc.sync.dma_start(out[:, c * P : (c + 1) * P], res[:])

@@ -56,9 +56,8 @@ def tile_picked_sage_relu_e_kernel(tc, xT, w1, w2, gate, offs, pos1, pos2, pos3,
         for t in range(TILES):
             for s in range(PASSES):
                 nc.sync.dma_start(w1_raw[t, s][:], w1_rows[s][:, :, t * P : (t + 1) * P])
-                d = PASSES * t + s - 3
-                if 0 <= d < D:
-                    nc.sync.dma_start(pos_t[d][:], (pos1, pos2, pos3)[d])
+            for d in {1: (0,), 2: (1, 2)}.get(t, ()):
+                nc.sync.dma_start(pos_t[d][:], (pos1, pos2, pos3)[d])
         nc.sync.dma_start(w2_raw[:], w2.rearrange("(p j) m -> p j m", j=PACK))
 
         ident = keep.tile([P, P], F32, name="ident")
@@ -114,6 +113,19 @@ def tile_picked_sage_relu_e_kernel(tc, xT, w1, w2, gate, offs, pos1, pos2, pos3,
         quantize_x(0, 0, S)
         for j in (1, 2):
             nc.vector.tensor_copy(x_grouped[1][:, :, j], plane[1, j].indirect(offs_t[:]))
+        warm_scales = keep.tile([P, P], U8, name="warm_scales", tag="x1_2", align_bytes=GRID)
+        nc.gpsimd.tensor_copy(warm_scales[:], x_scales[0][:, 0:P])
+        warm = psum.tile([P, S], F32, name="warm", tag="z1")
+        for i in range(2):
+            nc.tensor.matmul_mx(
+                out=warm[:],
+                lhsT=x_codes[0][:, 0:P].bitcast(FP8X4),
+                lhsT_scale=warm_scales[:],
+                rhs=x_codes[0][:].bitcast(FP8X4),
+                rhs_scale=x_scales[0][:],
+                start=True,
+                stop=True,
+            )
         for s in range(PASSES):
             round_w1(nc.scalar.copy, 0, s)
         for c0 in (0, half):
@@ -125,7 +137,7 @@ def tile_picked_sage_relu_e_kernel(tc, xT, w1, w2, gate, offs, pos1, pos2, pos3,
         quantize_w1(0, 1)
         quantize_x(1, S - P, S)
 
-        h = [keep.tile([P, S], F32, name=f"h{t}", align_bytes=GRID) if t not in (1, 2) else late.tile([P, S], F32, name=f"h{t}", offset=(4 * (t - 1) + 2) * KIB, align_bytes=GRID) for t in range(TILES)]
+        h = [keep.tile([P, S], F32, name=f"h{t}", align_bytes=GRID) if t not in (1, 2) else late.tile([P, S], F32, name=f"h{t}", offset=(4 * (t - 1) + 2) * KIB + (t - 1) * GRID, align_bytes=GRID) for t in range(TILES)]
 
         def first_layer(t, banks):
             width = S // len(banks)
@@ -147,7 +159,6 @@ def tile_picked_sage_relu_e_kernel(tc, xT, w1, w2, gate, offs, pos1, pos2, pos3,
                 else:
                     nc.scalar.activation(h[t][:, i * width : (i + 1) * width], acc[:], RELU)
 
-        w2_grouped = keep.tile([P, N, PACK], BF16, name="w2g", align_bytes=GRID)
         w2_scales = keep.tile([P, N], U8, name="w2_scales", align_bytes=GRID)
 
         round_w1(nc.scalar.copy, 1, 0)
@@ -164,14 +175,18 @@ def tile_picked_sage_relu_e_kernel(tc, xT, w1, w2, gate, offs, pos1, pos2, pos3,
             quantize_w1(t, 1)
         first_layer(2, ("hD",))
         first_layer(3, ("hA",))
+        w2_grouped = keep.tile([P, N, PACK], BF16, name="w2g", tag="w1_codes3_1", align_bytes=GRID)
         nc.scalar.copy(*interleave(w2_grouped[:], w2_raw[:]))
 
-        z_turned = [keep.tile([P, 2, P, 2], BF16, name=f"zt{c}", tag=buffer, align_bytes=GRID) for c, buffer in enumerate(("w2_raw", "w1g3_1"))]
+        z_turned = [
+            late.tile([P, 2, P, 2], BF16, name="zt0", offset=5 * KIB + GRID, align_bytes=GRID),
+            keep.tile([P, 2, P, 2], BF16, name="zt1", tag="w1g3_1", align_bytes=GRID),
+        ]
         term = {}
 
         def make_terms(t, d, n, buffer):
             if buffer in ("w1_raw2_1", "w1_raw3_1"):
-                terms = late.tile([P, n, V], F32, name=f"u{t}_{d}", offset=(4 * t + 2 - n) * KIB, align_bytes=GRID)
+                terms = late.tile([P, n, V], F32, name=f"u{t}_{d}", offset=(0, 4 * KIB + GRID)[t], align_bytes=GRID)
             else:
                 terms = keep.tile([P, n, V], F32, name=f"u{t}_{d}", tag=buffer, align_bytes=GRID)
             for i in range(n):
@@ -191,8 +206,8 @@ def tile_picked_sage_relu_e_kernel(tc, xT, w1, w2, gate, offs, pos1, pos2, pos3,
 
         for t in range(2):
             for d in range(D):
-                if t == 0 and d == 0:
-                    make_terms(t, d, 1, "u0")
+                if (t, d) in ((0, 0), (1, 1)):
+                    make_terms(t, d, 1, f"u{t}")
                 elif d > 0:
                     with_next_tile = 1 if (t, d) == (0, D - 1) else 0
                     make_terms(t, d, 1 + with_next_tile, f"w1_raw{t + 2}_{d - 1}")

@@ -12,8 +12,15 @@ HALVES = V // P
 LIST_ROWS = 16
 LINE = 4
 RUN = 8
-KIB = 1024
 GRID = 256
+KIB = 1024
+WARM_UPS = 2
+
+LATE_PIECE = {2: 1 * KIB, 3: 5 * KIB}
+LATE_TERMS = {0: 0, 1: 4 * KIB + GRID}
+LATE_HIDDEN = {1: 2 * KIB, 2: 6 * KIB + GRID}
+LATE_Z = 5 * KIB + GRID
+
 FLOPS = 2 * K * S * H + 2 * H * V * N
 
 F32 = mybir.dt.float32
@@ -39,11 +46,16 @@ def tile_picked_sage_relu_e_kernel(tc, xT, w1, w2, gate, offs, pos1, pos2, pos3,
         x_rows = xT.rearrange("(s p j) t -> s p j t", p=P, j=PACK)
         w1_rows = w1.rearrange("(s p j) c -> s p j c", p=P, j=PACK)
         x_loads = [[(0, 2), (2, 1), (3, 1)], [(j, 1) for j in range(PACK)]]
-        w1_raw = {(t, s): keep.tile([P, PACK, P], F32, name=f"w1_raw{t}_{s}", align_bytes=GRID) for t in range(TILES) for s in range(PASSES) if t < 2 or s == 0}
-        for t in (2, 3):
-            w1_raw[t, 1] = late.tile([P, PACK, P], F32, name=f"w1_raw{t}_1", offset=(4 * (t - 2) + 1) * KIB, align_bytes=GRID)
+        lists_after_tile = {1: (0,), 2: (1, 2)}
+        w1_raw = {
+            (t, s): keep.tile([P, PACK, P], F32, name=f"w1_raw{t}_{s}", align_bytes=GRID)
+            for t in range(TILES)
+            for s in range(PASSES)
+            if s == 0 or t not in LATE_PIECE
+        }
+        for t, offset in LATE_PIECE.items():
+            w1_raw[t, 1] = late.tile([P, PACK, P], F32, name=f"w1_raw{t}_1", offset=offset, align_bytes=GRID)
         w2_raw = keep.tile([P, PACK, N], F32, name="w2_raw", align_bytes=GRID)
-        gates = [keep.tile([P, V], F32, name=f"gates{d}", align_bytes=GRID) for d in range(D)]
         plane = {}
         for s in range(PASSES):
             for j0, n in x_loads[s]:
@@ -56,7 +68,7 @@ def tile_picked_sage_relu_e_kernel(tc, xT, w1, w2, gate, offs, pos1, pos2, pos3,
         for t in range(TILES):
             for s in range(PASSES):
                 nc.sync.dma_start(w1_raw[t, s][:], w1_rows[s][:, :, t * P : (t + 1) * P])
-            for d in {1: (0,), 2: (1, 2)}.get(t, ()):
+            for d in lists_after_tile.get(t, ()):
                 nc.sync.dma_start(pos_t[d][:], (pos1, pos2, pos3)[d])
         nc.sync.dma_start(w2_raw[:], w2.rearrange("(p j) m -> p j m", j=PACK))
 
@@ -68,7 +80,10 @@ def tile_picked_sage_relu_e_kernel(tc, xT, w1, w2, gate, offs, pos1, pos2, pos3,
         nc.gpsimd.memset(gate_cols[32:64], 0.0)
         nc.gpsimd.memset(gate_cols[64:P], 0.0)
 
-        for d, banks in enumerate((("hA", "hB"), ("hC", "hD"), ("z0", "z1"))):
+        gates = []
+
+        def spread_gate(d, banks, buffer):
+            gates.append(keep.tile([P, V], F32, name=f"gates{d}", tag=buffer, align_bytes=GRID))
             for b, bank in enumerate(banks):
                 spread = psum.tile([P, LINE, P], F32, name=f"gate_spread{d}_{b}", tag=bank)
                 for i in range(LINE):
@@ -77,10 +92,18 @@ def tile_picked_sage_relu_e_kernel(tc, xT, w1, w2, gate, offs, pos1, pos2, pos3,
                 dst = gates[d][:].rearrange("p (q i) -> p q i", i=RUN)[:, :, LINE * b : LINE * (b + 1)]
                 nc.scalar.copy(dst, spread[:, :, 0 : V // RUN].rearrange("p i q -> p q i"))
 
+        spread_gate(0, ("hA", "hB"), "gates0")
+        spread_gate(1, ("hC", "hD"), "gates1")
+
         x_grouped = [keep.tile([P, S, PACK], BF16, name=f"xg{s}", align_bytes=GRID) for s in range(PASSES)]
         x_codes = []
         x_scales = [keep.tile([P, S], U8, name=f"x_scales{s}", align_bytes=GRID) for s in range(PASSES)]
-        w1_grouped = {(t, s): keep.tile([P, P * PACK], BF16, name=f"w1g{t}_{s}", align_bytes=GRID) for t in range(TILES) for s in range(PASSES) if (t, s) != (3, 0)}
+        w1_grouped = {
+            (t, s): keep.tile([P, P * PACK], BF16, name=f"w1g{t}_{s}", align_bytes=GRID)
+            for t in range(TILES)
+            for s in range(PASSES)
+            if (t, s) != (3, 0)
+        }
         w1_codes = {}
         w1_scales = [keep.tile([P, PASSES * P], U8, name=f"w1_scales{t}", align_bytes=GRID) for t in range(TILES)]
 
@@ -113,14 +136,13 @@ def tile_picked_sage_relu_e_kernel(tc, xT, w1, w2, gate, offs, pos1, pos2, pos3,
         quantize_x(0, 0, S)
         for j in (1, 2):
             nc.vector.tensor_copy(x_grouped[1][:, :, j], plane[1, j].indirect(offs_t[:]))
-        warm_scales = keep.tile([P, P], U8, name="warm_scales", tag="x1_2", align_bytes=GRID)
-        nc.gpsimd.tensor_copy(warm_scales[:], x_scales[0][:, 0:P])
-        warm = psum.tile([P, S], F32, name="warm", tag="z1")
-        for i in range(2):
+        spread_gate(2, ("z0", "z1"), "x1_2")
+        warm = psum.tile([P, S], F32, name="warm", tag="z0")
+        for i in range(WARM_UPS):
             nc.tensor.matmul_mx(
                 out=warm[:],
                 lhsT=x_codes[0][:, 0:P].bitcast(FP8X4),
-                lhsT_scale=warm_scales[:],
+                lhsT_scale=x_scales[0][:, 0:P],
                 rhs=x_codes[0][:].bitcast(FP8X4),
                 rhs_scale=x_scales[0][:],
                 start=True,
@@ -129,7 +151,8 @@ def tile_picked_sage_relu_e_kernel(tc, xT, w1, w2, gate, offs, pos1, pos2, pos3,
         for s in range(PASSES):
             round_w1(nc.scalar.copy, 0, s)
         for c0 in (0, half):
-            nc.vector.tensor_copy(x_grouped[1][:, c0 : c0 + half, 3], plane[1, 3].indirect(offs_t[:, c0 // LIST_ROWS : (c0 + half) // LIST_ROWS]))
+            offsets = offs_t[:, c0 // LIST_ROWS : (c0 + half) // LIST_ROWS]
+            nc.vector.tensor_copy(x_grouped[1][:, c0 : c0 + half, 3], plane[1, 3].indirect(offsets))
         x_codes.append(keep.tile([P, S], U32, name="x_codes1", tag="w1_raw0_0", align_bytes=GRID))
         quantize_w1(0, 0)
         quantize_x(1, 0, half)
@@ -137,58 +160,59 @@ def tile_picked_sage_relu_e_kernel(tc, xT, w1, w2, gate, offs, pos1, pos2, pos3,
         quantize_w1(0, 1)
         quantize_x(1, S - P, S)
 
-        h = [keep.tile([P, S], F32, name=f"h{t}", align_bytes=GRID) if t not in (1, 2) else late.tile([P, S], F32, name=f"h{t}", offset=(4 * (t - 1) + 2) * KIB + (t - 1) * GRID, align_bytes=GRID) for t in range(TILES)]
+        h = [
+            late.tile([P, S], F32, name=f"h{t}", offset=LATE_HIDDEN[t], align_bytes=GRID)
+            if t in LATE_HIDDEN
+            else keep.tile([P, S], F32, name=f"h{t}", align_bytes=GRID)
+            for t in range(TILES)
+        ]
 
-        def first_layer(t, banks):
-            width = S // len(banks)
-            accs = [psum.tile([P, width], F32, name=f"h_acc{t}_{bank}", tag=bank) for bank in banks]
+        def first_layer(t, groups):
+            accs = [psum.tile([P, c1 - c0], F32, name=f"h_acc{t}_{bank}", tag=bank) for bank, c0, c1 in groups]
             for s in range(PASSES):
-                for i, acc in enumerate(accs):
+                for acc, (bank, c0, c1) in zip(accs, groups):
                     nc.tensor.matmul_mx(
                         out=acc[:],
                         lhsT=w1_codes[t, s][:].bitcast(FP8X4),
                         lhsT_scale=w1_scales[t][:, s * P : (s + 1) * P],
-                        rhs=x_codes[s][:, i * width : (i + 1) * width].bitcast(FP8X4),
-                        rhs_scale=x_scales[s][:, i * width : (i + 1) * width],
+                        rhs=x_codes[s][:, c0:c1].bitcast(FP8X4),
+                        rhs_scale=x_scales[s][:, c0:c1],
                         start=(s == 0),
                         stop=(s == PASSES - 1),
                     )
-            for i, acc in enumerate(accs):
-                if t == 0:
-                    nc.vector.tensor_scalar_max(h[t][:, i * width : (i + 1) * width], acc[:], 0.0)
+            for acc, (bank, c0, c1) in zip(accs, groups):
+                if (t, c0) == (0, 0):
+                    nc.vector.tensor_scalar_max(h[t][:, c0:c1], acc[:], 0.0)
                 else:
-                    nc.scalar.activation(h[t][:, i * width : (i + 1) * width], acc[:], RELU)
+                    nc.scalar.activation(h[t][:, c0:c1], acc[:], RELU)
 
         w2_scales = keep.tile([P, N], U8, name="w2_scales", align_bytes=GRID)
 
         round_w1(nc.scalar.copy, 1, 0)
         round_w1(nc.vector.tensor_copy, 1, 1)
         quantize_w1(1, 0)
-        first_layer(0, ("hA", "hB", "z2", "z3"))
+        first_layer(0, (("hA", 0, half), ("z2", half, S - P), ("z3", S - P, S)))
         quantize_w1(1, 1, "w1_codes0_1")
-        first_layer(1, ("hC",))
+        first_layer(1, (("hC", 0, S),))
         w1_grouped[3, 0] = keep.tile([P, P * PACK], BF16, name="w1g3_0", tag="w1_codes0_1", align_bytes=GRID)
         for t in (2, 3):
             for s in range(PASSES):
                 round_w1(nc.scalar.copy, t, s)
             quantize_w1(t, 0, "w1g1_1" if t == 2 else None)
             quantize_w1(t, 1)
-        first_layer(2, ("hD",))
-        first_layer(3, ("hA",))
+        first_layer(2, (("hD", 0, S),))
+        first_layer(3, (("hA", 0, S),))
         w2_grouped = keep.tile([P, N, PACK], BF16, name="w2g", tag="w1_codes3_1", align_bytes=GRID)
         nc.scalar.copy(*interleave(w2_grouped[:], w2_raw[:]))
 
         z_turned = [
-            late.tile([P, 2, P, 2], BF16, name="zt0", offset=5 * KIB + GRID, align_bytes=GRID),
+            late.tile([P, 2, P, 2], BF16, name="zt0", offset=LATE_Z, align_bytes=GRID),
             keep.tile([P, 2, P, 2], BF16, name="zt1", tag="w1g3_1", align_bytes=GRID),
         ]
         term = {}
 
-        def make_terms(t, d, n, buffer):
-            if buffer in ("w1_raw2_1", "w1_raw3_1"):
-                terms = late.tile([P, n, V], F32, name=f"u{t}_{d}", offset=(0, 4 * KIB + GRID)[t], align_bytes=GRID)
-            else:
-                terms = keep.tile([P, n, V], F32, name=f"u{t}_{d}", tag=buffer, align_bytes=GRID)
+        def make_terms(t, d, n, pool, **place):
+            terms = pool.tile([P, n, V], F32, name=f"u{t}_{d}", align_bytes=GRID, **place)
             for i in range(n):
                 term[divmod(D * t + d + i, D)] = terms[:, i, :]
 
@@ -204,13 +228,13 @@ def tile_picked_sage_relu_e_kernel(tc, xT, w1, w2, gate, offs, pos1, pos2, pos3,
             q = P // PACK
             return z_turned[c][:, :, q * t : q * (t + 1), :], acc.rearrange("v (q a e) -> v a q e", a=2, e=2)
 
+        make_terms(0, 0, 1, keep, tag="u0")
+        make_terms(0, 1, 1, keep, tag="w1_raw2_0")
+        make_terms(0, 2, 2, late, offset=LATE_TERMS[0])
+        make_terms(1, 1, 1, keep, tag="u1")
+        make_terms(1, 2, 1, late, offset=LATE_TERMS[1])
         for t in range(2):
             for d in range(D):
-                if (t, d) in ((0, 0), (1, 1)):
-                    make_terms(t, d, 1, f"u{t}")
-                elif d > 0:
-                    with_next_tile = 1 if (t, d) == (0, D - 1) else 0
-                    make_terms(t, d, 1 + with_next_tile, f"w1_raw{t + 2}_{d - 1}")
                 fetch(t, d, 0, V)
             acc = psum.tile([P, HALVES, P], F32, name=f"z_acc{t}", tag=f"z{t}")
             for c in range(HALVES):
@@ -219,7 +243,7 @@ def tile_picked_sage_relu_e_kernel(tc, xT, w1, w2, gate, offs, pos1, pos2, pos3,
                 nc.scalar.copy(*z_views(t, c, acc[:, c, :]))
 
         accs = [psum.tile([P, P], F32, name=f"z_acc2_{c}", tag=bank) for c, bank in enumerate(("hB", "hC"))]
-        make_terms(2, 0, 2 * D, "u2")
+        make_terms(2, 0, 2 * D, keep, tag="u2")
         for d in range(D):
             fetch(2, d, 0, V)
         for c in range(HALVES):
@@ -231,7 +255,7 @@ def tile_picked_sage_relu_e_kernel(tc, xT, w1, w2, gate, offs, pos1, pos2, pos3,
                 fetch(3, d, c * P, (c + 1) * P)
             turn_and_add(3, c, accs[c][:], range(D))
 
-        w2_codes = keep.tile([P, N], U32, name="w2_codes", tag=f"gates{D - 1}", align_bytes=GRID)
+        w2_codes = keep.tile([P, N], U32, name="w2_codes", tag="x1_2", align_bytes=GRID)
         quantize(w2_codes[:], w2_scales[:], w2_grouped[:].rearrange("p m j -> p (m j)"))
 
         for c in range(HALVES):
@@ -254,9 +278,9 @@ def tile_picked_sage_relu_e_kernel(tc, xT, w1, w2, gate, offs, pos1, pos2, pos3,
             step = P // len(banks)
             for i, bank in enumerate(banks):
                 cols = slice(i * step, (i + 1) * step)
-                words = z_grouped[:, PACK * cols.start : PACK * cols.stop]
-                nc.scalar.copy(words.bitcast(F32).rearrange("p (v a) -> p v a", a=2), back[:, :, cols].rearrange("p a v -> p v a"))
-                quantize(z_codes[:, cols], z_scales[:, cols], words)
+                values = z_grouped[:, PACK * cols.start : PACK * cols.stop]
+                nc.scalar.copy(values.bitcast(F32).rearrange("p (v a) -> p v a", a=2), back[:, :, cols].rearrange("p a v -> p v a"))
+                quantize(z_codes[:, cols], z_scales[:, cols], values)
                 o_acc = psum.tile([P, step], F32, name=f"o_acc{bank}", tag=bank)
                 nc.tensor.matmul_mx(
                     out=o_acc[:],

@@ -131,11 +131,13 @@ def tile_picked_sage_relu_e_kernel(tc, xT, w1, w2, gate, offs, pos1, pos2, pos3,
         nc.scalar.copy(*interleave(x_grouped[0][:, 0:half, :], picked[:, :, 0:half]))
         nc.vector.tensor_copy(*interleave(x_grouped[0][:, half:S, :], picked[:, :, half:S]))
 
-        nc.vector.tensor_copy(x_grouped[1][:, :, 0], plane[1, 0].indirect(offs_t[:]))
+        pair = keep.tile([P, 2, S], F32, name="pair", align_bytes=GRID)
+        nc.vector.tensor_copy(pair[:, 0, :], plane[1, 0].indirect(offs_t[:]))
         x_codes.append(keep.tile([P, S], U32, name="x_codes0", tag="x1_0", align_bytes=GRID))
         quantize_x(0, 0, S)
-        for j in (1, 2):
-            nc.vector.tensor_copy(x_grouped[1][:, :, j], plane[1, j].indirect(offs_t[:]))
+        nc.vector.tensor_copy(pair[:, 1, :], plane[1, 1].indirect(offs_t[:]))
+        nc.scalar.copy(*interleave(x_grouped[1][:, :, 0:2], pair[:]))
+        nc.vector.tensor_copy(x_grouped[1][:, :, 2], plane[1, 2].indirect(offs_t[:]))
         spread_gate(2, ("z0", "z1"), "x1_2")
         warm = psum.tile([P, S], F32, name="warm", tag="z0")
         for i in range(WARM_UPS):

@@ -31,6 +31,7 @@ U8 = mybir.dt.uint8
 FP8X4 = mybir.dt.float8_e4m3fn_x4
 MULT = mybir.AluOpType.mult
 RELU = mybir.ActivationFunctionType.Relu
+COPY = mybir.ActivationFunctionType.Copy
 
 
 def tile_picked_sage_relu_e_kernel(tc, xT, w1, w2, gate, offs, pos1, pos2, pos3, out):
@@ -204,6 +205,9 @@ def tile_picked_sage_relu_e_kernel(tc, xT, w1, w2, gate, offs, pos1, pos2, pos3,
             quantize_w1(t, 1)
         first_layer(2, (("hD", 0, S),))
         first_layer(3, (("hA", 0, S),))
+        plain = [keep.tile([P, P], F32, name=f"plain{d}", align_bytes=GRID) for d in range(D)]
+        for d in range(D):
+            nc.scalar.activation(plain[d][:], h[3][:].indirect(pos_t[d][:, 0 : P // LIST_ROWS]), COPY)
         w2_grouped = keep.tile([P, N, PACK], BF16, name="w2g", tag="w1_codes3_1", align_bytes=GRID)
         nc.scalar.copy(*interleave(w2_grouped[:], w2_raw[:]))
 
@@ -245,17 +249,24 @@ def tile_picked_sage_relu_e_kernel(tc, xT, w1, w2, gate, offs, pos1, pos2, pos3,
                 nc.scalar.copy(*z_views(t, c, acc[:, c, :]))
 
         accs = [psum.tile([P, P], F32, name=f"z_acc2_{c}", tag=bank) for c, bank in enumerate(("hB", "hC"))]
-        make_terms(2, 0, 2 * D, keep, tag="u2")
+        make_terms(2, 0, D, keep, tag="u2")
         for d in range(D):
             fetch(2, d, 0, V)
         for c in range(HALVES):
             turn_and_add(2, c, accs[c][:], range(D))
             nc.scalar.copy(*z_views(2, c, accs[c][:]))
         accs = [psum.tile([P, P], F32, name=f"z_acc3_{c}", tag=bank) for c, bank in enumerate(("z2", "z3"))]
-        for c in range(HALVES):
+        first = keep.tile([P, D, P], F32, name="u3_first", align_bytes=GRID)
+        second = [keep.tile([P, P], F32, name="u3_second0", align_bytes=GRID)]
+        nc.vector.tensor_tensor(second[0][:], h[3][:].indirect(pos_t[0][:, P // LIST_ROWS :]), gates[0][:, P:V], MULT)
+        for d in range(D):
+            nc.vector.tensor_tensor(first[:, d, :], plain[d][:], gates[d][:, 0:P], MULT)
+        for d in (1, 2):
+            second.append(keep.tile([P, P], F32, name=f"u3_second{d}", tag=f"plain{d - 1}", align_bytes=GRID))
+            nc.vector.tensor_tensor(second[d][:], h[3][:].indirect(pos_t[d][:, P // LIST_ROWS :]), gates[d][:, P:V], MULT)
+        for c, parts in enumerate(([first[:, d, :] for d in range(D)], [u[:] for u in second])):
             for d in range(D):
-                fetch(3, d, c * P, (c + 1) * P)
-            turn_and_add(3, c, accs[c][:], range(D))
+                nc.tensor.matmul(accs[c][:], parts[d], ident[:], start=(d == 0), stop=(d == D - 1), is_transpose=True)
 
         w2_codes = keep.tile([P, N], U32, name="w2_codes", tag="x1_2", align_bytes=GRID)
         quantize(w2_codes[:], w2_scales[:], w2_grouped[:].rearrange("p m j -> p (m j)"))

@@ -82,19 +82,20 @@ def tile_picked_sage_relu_e_kernel(tc, xT, w1, w2, gate, offs, pos1, pos2, pos3,
         nc.gpsimd.memset(gate_cols[64:P], 0.0)
 
         gates = []
+        gates01 = keep.tile([P, 2, V], F32, name="gates01", align_bytes=GRID)
 
-        def spread_gate(d, banks, buffer):
-            gates.append(keep.tile([P, V], F32, name=f"gates{d}", tag=buffer, align_bytes=GRID))
+        def spread_gate(d, banks, dst_row):
+            gates.append(dst_row)
             for b, bank in enumerate(banks):
                 spread = psum.tile([P, LINE, P], F32, name=f"gate_spread{d}_{b}", tag=bank)
                 for i in range(LINE):
                     column = gate_cols[:, d, LINE * b + i : LINE * b + i + 1]
                     nc.tensor.transpose(spread[:, i, :], column.to_broadcast([P, P]), ident[:])
-                dst = gates[d][:].rearrange("p (q i) -> p q i", i=RUN)[:, :, LINE * b : LINE * (b + 1)]
+                dst = gates[d].rearrange("p (q i) -> p q i", i=RUN)[:, :, LINE * b : LINE * (b + 1)]
                 nc.scalar.copy(dst, spread[:, :, 0 : V // RUN].rearrange("p i q -> p q i"))
 
-        spread_gate(0, ("hA", "hB"), "gates0")
-        spread_gate(1, ("hC", "hD"), "gates1")
+        spread_gate(0, ("hA", "hB"), gates01[:, 0, :])
+        spread_gate(1, ("hC", "hD"), gates01[:, 1, :])
 
         x_grouped = [keep.tile([P, S, PACK], BF16, name=f"xg{s}", align_bytes=GRID) for s in range(PASSES)]
         x_codes = []
@@ -139,7 +140,8 @@ def tile_picked_sage_relu_e_kernel(tc, xT, w1, w2, gate, offs, pos1, pos2, pos3,
         nc.vector.tensor_copy(pair[:, 1, :], plane[1, 1].indirect(offs_t[:]))
         nc.scalar.copy(*interleave(x_grouped[1][:, :, 0:2], pair[:]))
         nc.vector.tensor_copy(x_grouped[1][:, :, 2], plane[1, 2].indirect(offs_t[:]))
-        spread_gate(2, ("z0", "z1"), "x1_2")
+        gates2 = keep.tile([P, V], F32, name="gates2", tag="x1_2", align_bytes=GRID)
+        spread_gate(2, ("z0", "z1"), gates2[:])
         warm = psum.tile([P, S], F32, name="warm", tag="z0")
         for i in range(WARM_UPS):
             nc.tensor.matmul_mx(
@@ -183,33 +185,30 @@ def tile_picked_sage_relu_e_kernel(tc, xT, w1, w2, gate, offs, pos1, pos2, pos3,
                         start=(s == 0),
                         stop=(s == PASSES - 1),
                     )
-            for acc, (bank, c0, c1) in zip(accs, groups):
-                if (t, c0) == (0, 0):
-                    nc.vector.tensor_scalar_max(h[t][:, c0:c1], acc[:], 0.0)
-                else:
-                    nc.scalar.activation(h[t][:, c0:c1], acc[:], RELU)
+            return [(h[t][:, c0:c1], acc[:]) for acc, (bank, c0, c1) in zip(accs, groups)]
+
+        def relu(groups):
+            for dst, acc in groups:
+                nc.scalar.activation(dst, acc, RELU)
 
         w2_scales = keep.tile([P, N], U8, name="w2_scales", align_bytes=GRID)
 
         round_w1(nc.scalar.copy, 1, 0)
         round_w1(nc.vector.tensor_copy, 1, 1)
         quantize_w1(1, 0)
-        first_layer(0, (("hA", 0, half), ("z2", half, S - P), ("z3", S - P, S)))
+        first, *others = first_layer(0, (("hA", 0, half), ("z2", half, S - P), ("z3", S - P, S)))
+        nc.vector.tensor_scalar_max(*first, 0.0)
+        relu(others)
         quantize_w1(1, 1, "w1_codes0_1")
-        first_layer(1, (("hC", 0, S),))
+        relu(first_layer(1, (("hC", 0, S),)))
         w1_grouped[3, 0] = keep.tile([P, P * PACK], BF16, name="w1g3_0", tag="w1_codes0_1", align_bytes=GRID)
         for t in (2, 3):
             for s in range(PASSES):
                 round_w1(nc.scalar.copy, t, s)
             quantize_w1(t, 0, "w1g1_1" if t == 2 else None)
             quantize_w1(t, 1)
-        first_layer(2, (("hD", 0, S),))
-        first_layer(3, (("hA", 0, S),))
-        plain = [keep.tile([P, P], F32, name=f"plain{d}", align_bytes=GRID) for d in range(D)]
-        for d in range(D):
-            nc.scalar.activation(plain[d][:], h[3][:].indirect(pos_t[d][:, 0 : P // LIST_ROWS]), COPY)
-        w2_grouped = keep.tile([P, N, PACK], BF16, name="w2g", tag="w1_codes3_1", align_bytes=GRID)
-        nc.scalar.copy(*interleave(w2_grouped[:], w2_raw[:]))
+        relu(first_layer(2, (("hD", 0, S),)))
+        sums3 = first_layer(3, (("hA", 0, S),))
 
         z_turned = [
             late.tile([P, 2, P, 2], BF16, name="zt0", offset=LATE_Z, align_bytes=GRID),
@@ -237,33 +236,54 @@ def tile_picked_sage_relu_e_kernel(tc, xT, w1, w2, gate, offs, pos1, pos2, pos3,
         make_terms(0, 0, 1, keep, tag="u0")
         make_terms(0, 1, 1, keep, tag="w1_raw2_0")
         make_terms(0, 2, 2, late, offset=LATE_TERMS[0])
-        make_terms(1, 1, 1, keep, tag="u1")
+        make_terms(1, 1, 1, keep, tag="w1_raw3_0")
         make_terms(1, 2, 1, late, offset=LATE_TERMS[1])
+        def gather(dst, t, d, v0, v1):
+            nc.scalar.activation(dst, h[t][:].indirect(pos_t[d][:, v0 // LIST_ROWS : v1 // LIST_ROWS]), COPY)
+
+        sums0 = psum.tile([P, HALVES, P], F32, name="z_acc0", tag="z0")
+        sums1 = [psum.tile([P, P], F32, name=f"z_acc1_{c}", tag=bank) for c, bank in enumerate(("z1", "z3"))]
         for t in range(2):
             for d in range(D):
                 fetch(t, d, 0, V)
-            acc = psum.tile([P, HALVES, P], F32, name=f"z_acc{t}", tag=f"z{t}")
-            for c in range(HALVES):
-                turn_and_add(t, c, acc[:, c, :], reversed(range(D)))
-            for c in range(HALVES):
-                nc.scalar.copy(*z_views(t, c, acc[:, c, :]))
+        for c in range(HALVES):
+            turn_and_add(0, c, sums0[:, c, :], reversed(range(D)))
+        for c in range(HALVES):
+            turn_and_add(1, c, sums1[c][:], range(D))
+        for c in range(HALVES):
+            nc.scalar.copy(*z_views(0, c, sums0[:, c, :]))
+
+        plain22 = keep.tile([P, V], F32, name="plain22", align_bytes=GRID)
+        gather(plain22[:], 2, 2, 0, V)
+        relu(sums3)
+        plain01 = keep.tile([P, 2, P], F32, name="plain01", align_bytes=GRID)
+        plain2 = keep.tile([P, P], F32, name="plain2", align_bytes=GRID)
+        for d in range(2):
+            gather(plain01[:, d, :], 3, d, 0, P)
+        gather(plain2[:], 3, 2, 0, P)
+        for c in range(HALVES):
+            nc.scalar.copy(*z_views(1, c, sums1[c][:]))
 
         accs = [psum.tile([P, P], F32, name=f"z_acc2_{c}", tag=bank) for c, bank in enumerate(("hB", "hC"))]
         make_terms(2, 0, D, keep, tag="u2")
-        for d in range(D):
+        for d in range(2):
             fetch(2, d, 0, V)
+        nc.vector.tensor_tensor(term[2, 2], plain22[:], gates[2], MULT)
         for c in range(HALVES):
             turn_and_add(2, c, accs[c][:], range(D))
             nc.scalar.copy(*z_views(2, c, accs[c][:]))
+        w2_grouped = keep.tile([P, N, PACK], BF16, name="w2g", tag="plain22", align_bytes=GRID)
+        nc.scalar.copy(*interleave(w2_grouped[:], w2_raw[:]))
+
         accs = [psum.tile([P, P], F32, name=f"z_acc3_{c}", tag=bank) for c, bank in enumerate(("z2", "z3"))]
         first = keep.tile([P, D, P], F32, name="u3_first", align_bytes=GRID)
-        second = [keep.tile([P, P], F32, name="u3_second0", align_bytes=GRID)]
-        nc.vector.tensor_tensor(second[0][:], h[3][:].indirect(pos_t[0][:, P // LIST_ROWS :]), gates[0][:, P:V], MULT)
-        for d in range(D):
-            nc.vector.tensor_tensor(first[:, d, :], plain[d][:], gates[d][:, 0:P], MULT)
-        for d in (1, 2):
-            second.append(keep.tile([P, P], F32, name=f"u3_second{d}", tag=f"plain{d - 1}", align_bytes=GRID))
+        second = [keep.tile([P, P], F32, name=f"u3_second{d}", align_bytes=GRID) for d in range(2)]
+        for d in range(2):
             nc.vector.tensor_tensor(second[d][:], h[3][:].indirect(pos_t[d][:, P // LIST_ROWS :]), gates[d][:, P:V], MULT)
+        nc.vector.tensor_tensor(first[:, 0:2, :], plain01[:], gates01[:, :, 0:P], MULT)
+        nc.vector.tensor_tensor(first[:, 2, :], plain2[:], gates[2][:, 0:P], MULT)
+        second.append(keep.tile([P, P], F32, name="u3_second2", tag="plain01", align_bytes=GRID))
+        nc.vector.tensor_tensor(second[2][:], h[3][:].indirect(pos_t[2][:, P // LIST_ROWS :]), gates[2][:, P:V], MULT)
         for c, parts in enumerate(([first[:, d, :] for d in range(D)], [u[:] for u in second])):
             for d in range(D):
                 nc.tensor.matmul(accs[c][:], parts[d], ident[:], start=(d == 0), stop=(d == D - 1), is_transpose=True)
@@ -271,6 +291,7 @@ def tile_picked_sage_relu_e_kernel(tc, xT, w1, w2, gate, offs, pos1, pos2, pos3,
         w2_codes = keep.tile([P, N], U32, name="w2_codes", tag="x1_2", align_bytes=GRID)
         quantize(w2_codes[:], w2_scales[:], w2_grouped[:].rearrange("p m j -> p (m j)"))
 
+        backs = []
         for c in range(HALVES):
             copy = nc.scalar.copy if c == 0 else nc.vector.tensor_copy
             dst, src = z_views(3, c, accs[c][:])
@@ -283,6 +304,9 @@ def tile_picked_sage_relu_e_kernel(tc, xT, w1, w2, gate, offs, pos1, pos2, pos3,
             pairs = z_turned[c][:].rearrange("v a p e -> v (a p e)").bitcast(F32)
             for a in range(2):
                 nc.tensor.transpose(back[:, a, :], pairs[:, a * P : (a + 1) * P], ident[:])
+            backs.append(back)
+        for c, back in enumerate(backs):
+            copy = nc.scalar.copy if c == 0 else nc.vector.tensor_copy
             z_grouped = keep.tile([P, P * PACK], BF16, name=f"zg{c}", align_bytes=GRID)
             z_codes = keep.tile([P, P], U32, name=f"z_codes{c}", align_bytes=GRID)
             z_scales = keep.tile([P, P], U8, name=f"z_scales{c}", align_bytes=GRID)

@@ -14,7 +14,6 @@ LINE = 4
 RUN = 8
 GRID = 256
 KIB = 1024
-WARM_UPS = 2
 
 LATE_PIECE = {2: 1 * KIB, 3: 5 * KIB}
 LATE_TERMS = {0: 0, 1: 4 * KIB + GRID}
@@ -46,7 +45,7 @@ def tile_picked_sage_relu_e_kernel(tc, xT, w1, w2, gate, offs, pos1, pos2, pos3,
 
         x_rows = xT.rearrange("(s p j) t -> s p j t", p=P, j=PACK)
         w1_rows = w1.rearrange("(s p j) c -> s p j c", p=P, j=PACK)
-        x_loads = [[(0, 2), (2, 1), (3, 1)], [(j, 1) for j in range(PACK)]]
+        x_loads = [[(0, PACK)], [(j, 1) for j in range(PACK)]]
         lists_after_tile = {1: (0,), 2: (1, 2)}
         w1_raw = {
             (t, s): keep.tile([P, PACK, P], F32, name=f"w1_raw{t}_{s}", align_bytes=GRID)
@@ -79,10 +78,9 @@ def tile_picked_sage_relu_e_kernel(tc, xT, w1, w2, gate, offs, pos1, pos2, pos3,
         gate_cols = keep.tile([P, D, RUN], F32, name="gate_cols")
         nc.scalar.dma_start(gate_cols[0 : V // RUN], gate[:, 0, :].rearrange("d (q i) -> q d i", i=RUN))
         nc.gpsimd.memset(gate_cols[32:64], 0.0)
-        nc.gpsimd.memset(gate_cols[64:P], 0.0)
+        nc.scalar.activation(gate_cols[64:P].rearrange("p d i -> p (d i)"), ident[64:P, 0 : D * RUN], COPY, scale=0.0)
 
         gates = []
-        gates01 = keep.tile([P, 2, V], F32, name="gates01", align_bytes=GRID)
 
         def spread_gate(d, banks, dst_row):
             gates.append(dst_row)
@@ -94,8 +92,6 @@ def tile_picked_sage_relu_e_kernel(tc, xT, w1, w2, gate, offs, pos1, pos2, pos3,
                 dst = gates[d].rearrange("p (q i) -> p q i", i=RUN)[:, :, LINE * b : LINE * (b + 1)]
                 nc.scalar.copy(dst, spread[:, :, 0 : V // RUN].rearrange("p i q -> p q i"))
 
-        spread_gate(0, ("hA", "hB"), gates01[:, 0, :])
-        spread_gate(1, ("hC", "hD"), gates01[:, 1, :])
 
         x_grouped = [keep.tile([P, S, PACK], BF16, name=f"xg{s}", align_bytes=GRID) for s in range(PASSES)]
         x_codes = []
@@ -128,31 +124,24 @@ def tile_picked_sage_relu_e_kernel(tc, xT, w1, w2, gate, offs, pos1, pos2, pos3,
 
         half = S // 2
         picked = keep.tile([P, PACK, S], F32, name="picked", align_bytes=GRID)
-        for j in range(PACK):
+        for j in range(0, PACK, 2):
             nc.vector.tensor_copy(picked[:, j, :], plane[0, j].indirect(offs_t[:]))
+            nc.scalar.activation(picked[:, j + 1, :], plane[0, j + 1].indirect(offs_t[:]), COPY)
         nc.scalar.copy(*interleave(x_grouped[0][:, 0:half, :], picked[:, :, 0:half]))
         nc.vector.tensor_copy(*interleave(x_grouped[0][:, half:S, :], picked[:, :, half:S]))
 
-        pair = keep.tile([P, 2, S], F32, name="pair", align_bytes=GRID)
+        pair = keep.tile([P, 2, S], F32, name="pair", tag="x0_0", align_bytes=GRID)
         nc.vector.tensor_copy(pair[:, 0, :], plane[1, 0].indirect(offs_t[:]))
         x_codes.append(keep.tile([P, S], U32, name="x_codes0", tag="x1_0", align_bytes=GRID))
         quantize_x(0, 0, S)
-        nc.vector.tensor_copy(pair[:, 1, :], plane[1, 1].indirect(offs_t[:]))
-        nc.scalar.copy(*interleave(x_grouped[1][:, :, 0:2], pair[:]))
+        nc.scalar.activation(pair[:, 1, :], plane[1, 1].indirect(offs_t[:]), COPY)
+        nc.vector.tensor_copy(*interleave(x_grouped[1][:, :, 0:2], pair[:]))
+        gates01 = keep.tile([P, 2, V], F32, name="gates01", tag="x0_0", align_bytes=GRID)
+        spread_gate(0, ("hA", "hB"), gates01[:, 0, :])
+        spread_gate(1, ("hC", "hD"), gates01[:, 1, :])
         nc.vector.tensor_copy(x_grouped[1][:, :, 2], plane[1, 2].indirect(offs_t[:]))
         gates2 = keep.tile([P, V], F32, name="gates2", tag="x1_2", align_bytes=GRID)
         spread_gate(2, ("z0", "z1"), gates2[:])
-        warm = psum.tile([P, S], F32, name="warm", tag="z0")
-        for i in range(WARM_UPS):
-            nc.tensor.matmul_mx(
-                out=warm[:],
-                lhsT=x_codes[0][:, 0:P].bitcast(FP8X4),
-                lhsT_scale=x_scales[0][:, 0:P],
-                rhs=x_codes[0][:].bitcast(FP8X4),
-                rhs_scale=x_scales[0][:],
-                start=True,
-                stop=True,
-            )
         for s in range(PASSES):
             round_w1(nc.scalar.copy, 0, s)
         for c0 in (0, half):
@@ -242,7 +231,7 @@ def tile_picked_sage_relu_e_kernel(tc, xT, w1, w2, gate, offs, pos1, pos2, pos3,
             nc.scalar.activation(dst, h[t][:].indirect(pos_t[d][:, v0 // LIST_ROWS : v1 // LIST_ROWS]), COPY)
 
         sums0 = psum.tile([P, HALVES, P], F32, name="z_acc0", tag="z0")
-        sums1 = [psum.tile([P, P], F32, name=f"z_acc1_{c}", tag=bank) for c, bank in enumerate(("z1", "z3"))]
+        sums1 = [psum.tile([P, P], F32, name=f"z_acc1_{c}", tag=bank) for c, bank in enumerate(("z1", "hA"))]
         for t in range(2):
             for d in range(D):
                 fetch(t, d, 0, V)
@@ -256,11 +245,10 @@ def tile_picked_sage_relu_e_kernel(tc, xT, w1, w2, gate, offs, pos1, pos2, pos3,
         plain22 = keep.tile([P, V], F32, name="plain22", align_bytes=GRID)
         gather(plain22[:], 2, 2, 0, V)
         relu(sums3)
-        plain01 = keep.tile([P, 2, P], F32, name="plain01", align_bytes=GRID)
-        plain2 = keep.tile([P, P], F32, name="plain2", align_bytes=GRID)
-        for d in range(2):
-            gather(plain01[:, d, :], 3, d, 0, P)
-        gather(plain2[:], 3, 2, 0, P)
+        by_scalar = ((0, 0), (1, 0), (1, 1))
+        plain = keep.tile([P, len(by_scalar), P], F32, name="plain", align_bytes=GRID)
+        for i, (c, d) in enumerate(by_scalar):
+            gather(plain[:, i, :], 3, d, c * P, (c + 1) * P)
         for c in range(HALVES):
             nc.scalar.copy(*z_views(1, c, sums1[c][:]))
 
@@ -276,17 +264,17 @@ def tile_picked_sage_relu_e_kernel(tc, xT, w1, w2, gate, offs, pos1, pos2, pos3,
         nc.scalar.copy(*interleave(w2_grouped[:], w2_raw[:]))
 
         accs = [psum.tile([P, P], F32, name=f"z_acc3_{c}", tag=bank) for c, bank in enumerate(("z2", "z3"))]
-        first = keep.tile([P, D, P], F32, name="u3_first", align_bytes=GRID)
-        second = [keep.tile([P, P], F32, name=f"u3_second{d}", align_bytes=GRID) for d in range(2)]
-        for d in range(2):
-            nc.vector.tensor_tensor(second[d][:], h[3][:].indirect(pos_t[d][:, P // LIST_ROWS :]), gates[d][:, P:V], MULT)
-        nc.vector.tensor_tensor(first[:, 0:2, :], plain01[:], gates01[:, :, 0:P], MULT)
-        nc.vector.tensor_tensor(first[:, 2, :], plain2[:], gates[2][:, 0:P], MULT)
-        second.append(keep.tile([P, P], F32, name="u3_second2", tag="plain01", align_bytes=GRID))
-        nc.vector.tensor_tensor(second[2][:], h[3][:].indirect(pos_t[2][:, P // LIST_ROWS :]), gates[2][:, P:V], MULT)
-        for c, parts in enumerate(([first[:, d, :] for d in range(D)], [u[:] for u in second])):
-            for d in range(D):
-                nc.tensor.matmul(accs[c][:], parts[d], ident[:], start=(d == 0), stop=(d == D - 1), is_transpose=True)
+        terms3 = keep.tile([P, HALVES, D, P], F32, name="u3", align_bytes=GRID)
+        for c, turns in enumerate(((2, 1, 0), (2, 0, 1))):
+            cols = slice(c * P, (c + 1) * P)
+            for d in turns:
+                if (c, d) in by_scalar:
+                    values = plain[:, by_scalar.index((c, d)), :]
+                else:
+                    values = h[3][:].indirect(pos_t[d][:, cols.start // LIST_ROWS : cols.stop // LIST_ROWS])
+                nc.vector.tensor_tensor(terms3[:, c, d, :], values, gates[d][:, cols], MULT)
+            for i, d in enumerate(turns):
+                nc.tensor.matmul(accs[c][:], terms3[:, c, d, :], ident[:], start=(i == 0), stop=(i == D - 1), is_transpose=True)
 
         w2_codes = keep.tile([P, N], U32, name="w2_codes", tag="x1_2", align_bytes=GRID)
         quantize(w2_codes[:], w2_scales[:], w2_grouped[:].rearrange("p m j -> p (m j)"))

@@ -45,7 +45,7 @@ def tile_picked_sage_relu_e_kernel(tc, xT, w1, w2, gate, offs, pos1, pos2, pos3,
 
         x_rows = xT.rearrange("(s p j) t -> s p j t", p=P, j=PACK)
         w1_rows = w1.rearrange("(s p j) c -> s p j c", p=P, j=PACK)
-        x_loads = [[(0, PACK)], [(j, 1) for j in range(PACK)]]
+        x_loads = [[(0, 2), (2, 1), (3, 1)], [(j, 1) for j in range(PACK)]]
         lists_after_tile = {1: (0,), 2: (1, 2)}
         w1_raw = {
             (t, s): keep.tile([P, PACK, P], F32, name=f"w1_raw{t}_{s}", align_bytes=GRID)
@@ -78,9 +78,10 @@ def tile_picked_sage_relu_e_kernel(tc, xT, w1, w2, gate, offs, pos1, pos2, pos3,
         gate_cols = keep.tile([P, D, RUN], F32, name="gate_cols")
         nc.scalar.dma_start(gate_cols[0 : V // RUN], gate[:, 0, :].rearrange("d (q i) -> q d i", i=RUN))
         nc.gpsimd.memset(gate_cols[32:64], 0.0)
-        nc.scalar.activation(gate_cols[64:P].rearrange("p d i -> p (d i)"), ident[64:P, 0 : D * RUN], COPY, scale=0.0)
+        nc.gpsimd.memset(gate_cols[64:P], 0.0)
 
         gates = []
+        gates01 = keep.tile([P, 2, V], F32, name="gates01", align_bytes=GRID)
 
         def spread_gate(d, banks, dst_row):
             gates.append(dst_row)
@@ -92,6 +93,8 @@ def tile_picked_sage_relu_e_kernel(tc, xT, w1, w2, gate, offs, pos1, pos2, pos3,
                 dst = gates[d].rearrange("p (q i) -> p q i", i=RUN)[:, :, LINE * b : LINE * (b + 1)]
                 nc.scalar.copy(dst, spread[:, :, 0 : V // RUN].rearrange("p i q -> p q i"))
 
+        spread_gate(0, ("hA", "hB"), gates01[:, 0, :])
+        spread_gate(1, ("hC", "hD"), gates01[:, 1, :])
 
         x_grouped = [keep.tile([P, S, PACK], BF16, name=f"xg{s}", align_bytes=GRID) for s in range(PASSES)]
         x_codes = []
@@ -124,21 +127,17 @@ def tile_picked_sage_relu_e_kernel(tc, xT, w1, w2, gate, offs, pos1, pos2, pos3,
 
         half = S // 2
         picked = keep.tile([P, PACK, S], F32, name="picked", align_bytes=GRID)
-        for j in range(0, PACK, 2):
+        for j in range(PACK):
             nc.vector.tensor_copy(picked[:, j, :], plane[0, j].indirect(offs_t[:]))
-            nc.scalar.activation(picked[:, j + 1, :], plane[0, j + 1].indirect(offs_t[:]), COPY)
         nc.scalar.copy(*interleave(x_grouped[0][:, 0:half, :], picked[:, :, 0:half]))
         nc.vector.tensor_copy(*interleave(x_grouped[0][:, half:S, :], picked[:, :, half:S]))
 
-        pair = keep.tile([P, 2, S], F32, name="pair", tag="x0_0", align_bytes=GRID)
+        pair = keep.tile([P, 2, S], F32, name="pair", align_bytes=GRID)
         nc.vector.tensor_copy(pair[:, 0, :], plane[1, 0].indirect(offs_t[:]))
         x_codes.append(keep.tile([P, S], U32, name="x_codes0", tag="x1_0", align_bytes=GRID))
         quantize_x(0, 0, S)
-        nc.scalar.activation(pair[:, 1, :], plane[1, 1].indirect(offs_t[:]), COPY)
-        nc.vector.tensor_copy(*interleave(x_grouped[1][:, :, 0:2], pair[:]))
-        gates01 = keep.tile([P, 2, V], F32, name="gates01", tag="x0_0", align_bytes=GRID)
-        spread_gate(0, ("hA", "hB"), gates01[:, 0, :])
-        spread_gate(1, ("hC", "hD"), gates01[:, 1, :])
+        nc.vector.tensor_copy(pair[:, 1, :], plane[1, 1].indirect(offs_t[:]))
+        nc.scalar.copy(*interleave(x_grouped[1][:, :, 0:2], pair[:]))
         nc.vector.tensor_copy(x_grouped[1][:, :, 2], plane[1, 2].indirect(offs_t[:]))
         gates2 = keep.tile([P, V], F32, name="gates2", tag="x1_2", align_bytes=GRID)
         spread_gate(2, ("z0", "z1"), gates2[:])
@@ -245,7 +244,7 @@ def tile_picked_sage_relu_e_kernel(tc, xT, w1, w2, gate, offs, pos1, pos2, pos3,
         plain22 = keep.tile([P, V], F32, name="plain22", align_bytes=GRID)
         gather(plain22[:], 2, 2, 0, V)
         relu(sums3)
-        by_scalar = ((0, 0), (1, 0), (1, 1))
+        by_scalar = ((0, 0), (1, 0), (1, 1), (1, 2))
         plain = keep.tile([P, len(by_scalar), P], F32, name="plain", align_bytes=GRID)
         for i, (c, d) in enumerate(by_scalar):
             gather(plain[:, i, :], 3, d, c * P, (c + 1) * P)
@@ -260,12 +259,10 @@ def tile_picked_sage_relu_e_kernel(tc, xT, w1, w2, gate, offs, pos1, pos2, pos3,
         for c in range(HALVES):
             turn_and_add(2, c, accs[c][:], range(D))
             nc.scalar.copy(*z_views(2, c, accs[c][:]))
-        w2_grouped = keep.tile([P, N, PACK], BF16, name="w2g", tag="plain22", align_bytes=GRID)
-        nc.scalar.copy(*interleave(w2_grouped[:], w2_raw[:]))
 
         accs = [psum.tile([P, P], F32, name=f"z_acc3_{c}", tag=bank) for c, bank in enumerate(("z2", "z3"))]
         terms3 = keep.tile([P, HALVES, D, P], F32, name="u3", align_bytes=GRID)
-        for c, turns in enumerate(((2, 1, 0), (2, 0, 1))):
+        for c, turns in enumerate(((2, 1, 0), (0, 1, 2))):
             cols = slice(c * P, (c + 1) * P)
             for d in turns:
                 if (c, d) in by_scalar:
@@ -276,8 +273,8 @@ def tile_picked_sage_relu_e_kernel(tc, xT, w1, w2, gate, offs, pos1, pos2, pos3,
             for i, d in enumerate(turns):
                 nc.tensor.matmul(accs[c][:], terms3[:, c, d, :], ident[:], start=(i == 0), stop=(i == D - 1), is_transpose=True)
 
-        w2_codes = keep.tile([P, N], U32, name="w2_codes", tag="x1_2", align_bytes=GRID)
-        quantize(w2_codes[:], w2_scales[:], w2_grouped[:].rearrange("p m j -> p (m j)"))
+        w2_grouped = keep.tile([P, N, PACK], BF16, name="w2g", tag="h3", align_bytes=GRID)
+        nc.vector.tensor_copy(*interleave(w2_grouped[:], w2_raw[:]))
 
         backs = []
         for c in range(HALVES):
@@ -293,6 +290,8 @@ def tile_picked_sage_relu_e_kernel(tc, xT, w1, w2, gate, offs, pos1, pos2, pos3,
             for a in range(2):
                 nc.tensor.transpose(back[:, a, :], pairs[:, a * P : (a + 1) * P], ident[:])
             backs.append(back)
+        w2_codes = keep.tile([P, N], U32, name="w2_codes", align_bytes=GRID)
+        quantize(w2_codes[:], w2_scales[:], w2_grouped[:].rearrange("p m j -> p (m j)"))
         for c, back in enumerate(backs):
             copy = nc.scalar.copy if c == 0 else nc.vector.tensor_copy
             z_grouped = keep.tile([P, P * PACK], BF16, name=f"zg{c}", align_bytes=GRID)

from contextlib import ExitStack

import concourse.mybir as mybir
from concourse.masks import make_identity

K, T, D, S, V, H, N = 1024, 2048, 3, 512, 256, 512, 128
P = 128
PACK = 4
PASSES = K // (P * PACK)
TILES = H // P
HALVES = V // P
LIST_ROWS = 16
LINE = 4
RUN = 8
GRID = 256
KIB = 1024

LATE_PIECE = {2: 1 * KIB, 3: 5 * KIB}
LATE_TERMS = {0: 0, 1: 4 * KIB + GRID}
LATE_HIDDEN = {1: 2 * KIB, 2: 6 * KIB + GRID}
LATE_Z = 5 * KIB + GRID

FLOPS = 2 * K * S * H + 2 * H * V * N

F32 = mybir.dt.float32
BF16 = mybir.dt.bfloat16
U32 = mybir.dt.uint32
U16 = mybir.dt.uint16
U8 = mybir.dt.uint8
FP8X4 = mybir.dt.float8_e4m3fn_x4
MULT = mybir.AluOpType.mult
RELU = mybir.ActivationFunctionType.Relu
COPY = mybir.ActivationFunctionType.Copy


def tile_picked_sage_relu_e_kernel(tc, xT, w1, w2, gate, offs, pos1, pos2, pos3, out):
    nc = tc.nc
    with ExitStack() as ctx:
        keep = ctx.enter_context(tc.tile_pool(name="keep", bufs=1))
        late = ctx.enter_context(tc.tile_pool(name="late", bufs=1))
        psum = ctx.enter_context(tc.psum_pool(name="psum", bufs=1))

        offs_t = keep.tile([P, S // LIST_ROWS], U16, name="offs_t")
        pos_t = [keep.tile([P, V // LIST_ROWS], U16, name=f"pos_t{d}") for d in range(D)]

        x_rows = xT.rearrange("(s p j) t -> s p j t", p=P, j=PACK)
        w1_rows = w1.rearrange("(s p j) c -> s p j c", p=P, j=PACK)
        x_loads = [[(0, 2), (2, 1), (3, 1)], [(j, 1) for j in range(PACK)]]
        lists_after_tile = {1: (0,), 2: (1, 2)}
        w1_raw = {
            (t, s): keep.tile([P, PACK, P], F32, name=f"w1_raw{t}_{s}", align_bytes=GRID)
            for t in range(TILES)
            for s in range(PASSES)
            if s == 0 or t not in LATE_PIECE
        }
        for t, offset in LATE_PIECE.items():
            w1_raw[t, 1] = late.tile([P, PACK, P], F32, name=f"w1_raw{t}_1", offset=offset, align_bytes=GRID)
        w2_raw = keep.tile([P, PACK, N], F32, name="w2_raw", align_bytes=GRID)
        plane = {}
        for s in range(PASSES):
            for j0, n in x_loads[s]:
                x_t = keep.tile([P, n, T], F32, name=f"x{s}_{j0}", align_bytes=GRID)
                nc.sync.dma_start(x_t[:], x_rows[s][:, j0 : j0 + n, :])
                if (s, j0) == (0, 0):
                    nc.sync.dma_start(offs_t[:], offs)
                for j in range(n):
                    plane[s, j0 + j] = x_t[:, j, :]
        for t in range(TILES):
            for s in range(PASSES):
                nc.sync.dma_start(w1_raw[t, s][:], w1_rows[s][:, :, t * P : (t + 1) * P])
            for d in lists_after_tile.get(t, ()):
                nc.sync.dma_start(pos_t[d][:], (pos1, pos2, pos3)[d])
        nc.sync.dma_start(w2_raw[:], w2.rearrange("(p j) m -> p j m", j=PACK))

        ident = keep.tile([P, P], F32, name="ident")
        make_identity(nc, ident[:])

        gate_cols = keep.tile([P, D, RUN], F32, name="gate_cols")
        nc.scalar.dma_start(gate_cols[0 : V // RUN], gate[:, 0, :].rearrange("d (q i) -> q d i", i=RUN))
        nc.gpsimd.memset(gate_cols[32:64], 0.0)
        nc.gpsimd.memset(gate_cols[64:P], 0.0)

        gates = []
        gates01 = keep.tile([P, 2, V], F32, name="gates01", align_bytes=GRID)

        def spread_gate(d, banks, dst_row):
            gates.append(dst_row)
            for b, bank in enumerate(banks):
                spread = psum.tile([P, LINE, P], F32, name=f"gate_spread{d}_{b}", tag=bank)
                for i in range(LINE):
                    column = gate_cols[:, d, LINE * b + i : LINE * b + i + 1]
                    nc.tensor.transpose(spread[:, i, :], column.to_broadcast([P, P]), ident[:])
                dst = gates[d].rearrange("p (q i) -> p q i", i=RUN)[:, :, LINE * b : LINE * (b + 1)]
                nc.scalar.copy(dst, spread[:, :, 0 : V // RUN].rearrange("p i q -> p q i"))

        spread_gate(0, ("hA", "hB"), gates01[:, 0, :])
        spread_gate(1, ("hC", "hD"), gates01[:, 1, :])

        x_grouped = [keep.tile([P, S, PACK], BF16, name=f"xg{s}", align_bytes=GRID) for s in range(PASSES)]
        x_codes = []
        x_scales = [keep.tile([P, S], U8, name=f"x_scales{s}", align_bytes=GRID) for s in range(PASSES)]
        w1_grouped = {
            (t, s): keep.tile([P, P * PACK], BF16, name=f"w1g{t}_{s}", align_bytes=GRID)
            for t in range(TILES)
            for s in range(PASSES)
            if (t, s) != (3, 0)
        }
        w1_codes = {}
        w1_scales = [keep.tile([P, PASSES * P], U8, name=f"w1_scales{t}", align_bytes=GRID) for t in range(TILES)]

        def quantize(codes, scales, grouped):
            nc.vector.quantize_mx(out=codes.bitcast(FP8X4), scales=scales, in_=grouped)

        def quantize_x(s, c0, c1):
            quantize(x_codes[s][:, c0:c1], x_scales[s][:, c0:c1], x_grouped[s][:, c0:c1, :].rearrange("p n j -> p (n j)"))

        def quantize_w1(t, s, buffer=None):
            name = f"w1_codes{t}_{s}"
            w1_codes[t, s] = keep.tile([P, P], U32, name=name, tag=buffer or name, align_bytes=GRID)
            quantize(w1_codes[t, s][:], w1_scales[t][:, s * P : (s + 1) * P], w1_grouped[t, s][:])

        def interleave(dst, src):
            return dst.rearrange("p (c i) j -> p c j i", i=LINE), src.rearrange("p j (c i) -> p c j i", i=LINE)

        def round_w1(copy, t, s):
            copy(*interleave(w1_grouped[t, s][:].rearrange("p (m j) -> p m j", j=PACK), w1_raw[t, s][:]))

        half = S // 2
        picked = keep.tile([P, PACK, S], F32, name="picked", align_bytes=GRID)
        for j in range(PACK):
            nc.vector.tensor_copy(picked[:, j, :], plane[0, j].indirect(offs_t[:]))
        nc.scalar.copy(*interleave(x_grouped[0][:, 0:half, :], picked[:, :, 0:half]))
        nc.vector.tensor_copy(*interleave(x_grouped[0][:, half:S, :], picked[:, :, half:S]))

        pair = keep.tile([P, 2, S], F32, name="pair", align_bytes=GRID)
        nc.vector.tensor_copy(pair[:, 0, :], plane[1, 0].indirect(offs_t[:]))
        x_codes.append(keep.tile([P, S], U32, name="x_codes0", tag="x1_0", align_bytes=GRID))
        quantize_x(0, 0, S)
        nc.vector.tensor_copy(pair[:, 1, :], plane[1, 1].indirect(offs_t[:]))
        nc.scalar.copy(*interleave(x_grouped[1][:, :, 0:2], pair[:]))
        nc.vector.tensor_copy(x_grouped[1][:, :, 2], plane[1, 2].indirect(offs_t[:]))
        gates2 = keep.tile([P, V], F32, name="gates2", tag="x1_2", align_bytes=GRID)
        spread_gate(2, ("z0", "z1"), gates2[:])
        for s in range(PASSES):
            round_w1(nc.scalar.copy, 0, s)
        for c0 in (0, half):
            offsets = offs_t[:, c0 // LIST_ROWS : (c0 + half) // LIST_ROWS]
            nc.vector.tensor_copy(x_grouped[1][:, c0 : c0 + half, 3], plane[1, 3].indirect(offsets))
        x_codes.append(keep.tile([P, S], U32, name="x_codes1", tag="w1_raw0_0", align_bytes=GRID))
        quantize_w1(0, 0)
        quantize_x(1, 0, half)
        quantize_x(1, half, S - P)
        quantize_w1(0, 1)
        quantize_x(1, S - P, S)

        h = [
            late.tile([P, S], F32, name=f"h{t}", offset=LATE_HIDDEN[t], align_bytes=GRID)
            if t in LATE_HIDDEN
            else keep.tile([P, S], F32, name=f"h{t}", align_bytes=GRID)
            for t in range(TILES)
        ]

        def first_layer(t, groups):
            accs = [psum.tile([P, c1 - c0], F32, name=f"h_acc{t}_{bank}", tag=bank) for bank, c0, c1 in groups]
            for s in range(PASSES):
                for acc, (bank, c0, c1) in zip(accs, groups):
                    nc.tensor.matmul_mx(
                        out=acc[:],
                        lhsT=w1_codes[t, s][:].bitcast(FP8X4),
                        lhsT_scale=w1_scales[t][:, s * P : (s + 1) * P],
                        rhs=x_codes[s][:, c0:c1].bitcast(FP8X4),
                        rhs_scale=x_scales[s][:, c0:c1],
                        start=(s == 0),
                        stop=(s == PASSES - 1),
                    )
            return [(h[t][:, c0:c1], acc[:]) for acc, (bank, c0, c1) in zip(accs, groups)]

        def relu(groups):
            for dst, acc in groups:
                nc.scalar.activation(dst, acc, RELU)

        w2_scales = keep.tile([P, N], U8, name="w2_scales", align_bytes=GRID)

        round_w1(nc.scalar.copy, 1, 0)
        round_w1(nc.vector.tensor_copy, 1, 1)
        quantize_w1(1, 0)
        first, *others = first_layer(0, (("hA", 0, half), ("z2", half, S - P), ("z3", S - P, S)))
        nc.vector.tensor_scalar_max(*first, 0.0)
        relu(others)
        quantize_w1(1, 1, "w1_codes0_1")
        relu(first_layer(1, (("hC", 0, S),)))
        w1_grouped[3, 0] = keep.tile([P, P * PACK], BF16, name="w1g3_0", tag="w1_codes0_1", align_bytes=GRID)
        for t in (2, 3):
            for s in range(PASSES):
                round_w1(nc.scalar.copy, t, s)
            quantize_w1(t, 0, "w1g1_1" if t == 2 else None)
            quantize_w1(t, 1)
        relu(first_layer(2, (("hD", 0, S),)))
        sums3 = first_layer(3, (("hA", 0, S),))

        z_turned = [
            late.tile([P, 2, P, 2], BF16, name="zt0", offset=LATE_Z, align_bytes=GRID),
            keep.tile([P, 2, P, 2], BF16, name="zt1", tag="w1g3_1", align_bytes=GRID),
        ]
        term = {}

        def make_terms(t, d, n, pool, **place):
            terms = pool.tile([P, n, V], F32, name=f"u{t}_{d}", align_bytes=GRID, **place)
            for i in range(n):
                term[divmod(D * t + d + i, D)] = terms[:, i, :]

        def fetch(t, d, v0, v1):
            offsets = pos_t[d][:, v0 // LIST_ROWS : v1 // LIST_ROWS]
            nc.vector.tensor_tensor(term[t, d][:, v0:v1], h[t][:].indirect(offsets), gates[d][:, v0:v1], MULT)

        def turn_and_add(t, c, acc, turns):
            for i, d in enumerate(turns):
                nc.tensor.matmul(acc, term[t, d][:, c * P : (c + 1) * P], ident[:], start=(i == 0), stop=(i == D - 1), is_transpose=True)

        def z_views(t, c, acc):
            q = P // PACK
            return z_turned[c][:, :, q * t : q * (t + 1), :], acc.rearrange("v (q a e) -> v a q e", a=2, e=2)

        make_terms(0, 0, 1, keep, tag="u0")
        make_terms(0, 1, 1, keep, tag="w1_raw2_0")
        make_terms(0, 2, 2, late, offset=LATE_TERMS[0])
        make_terms(1, 1, 1, keep, tag="w1_raw3_0")
        make_terms(1, 2, 1, late, offset=LATE_TERMS[1])
        def gather(dst, t, d, v0, v1):
            nc.scalar.activation(dst, h[t][:].indirect(pos_t[d][:, v0 // LIST_ROWS : v1 // LIST_ROWS]), COPY)

        sums0 = psum.tile([P, HALVES, P], F32, name="z_acc0", tag="z0")
        sums1 = [psum.tile([P, P], F32, name=f"z_acc1_{c}", tag=bank) for c, bank in enumerate(("z1", "hA"))]
        for t in range(2):
            for d in range(D):
                fetch(t, d, 0, V)
        for c in range(HALVES):
            turn_and_add(0, c, sums0[:, c, :], reversed(range(D)))
        for c in range(HALVES):
            turn_and_add(1, c, sums1[c][:], range(D))
        for c in range(HALVES):
            nc.scalar.copy(*z_views(0, c, sums0[:, c, :]))

        plain22 = keep.tile([P, V], F32, name="plain22", align_bytes=GRID)
        gather(plain22[:], 2, 2, 0, V)
        relu(sums3)
        by_scalar = ((0, 0), (1, 0), (1, 1), (1, 2))
        plain = keep.tile([P, len(by_scalar), P], F32, name="plain", align_bytes=GRID)
        for i, (c, d) in enumerate(by_scalar):
            gather(plain[:, i, :], 3, d, c * P, (c + 1) * P)
        for c in range(HALVES):
            nc.scalar.copy(*z_views(1, c, sums1[c][:]))

        accs = [psum.tile([P, P], F32, name=f"z_acc2_{c}", tag=bank) for c, bank in enumerate(("hB", "hC"))]
        make_terms(2, 0, D, keep, tag="u2")
        for d in range(2):
            fetch(2, d, 0, V)
        nc.vector.tensor_tensor(term[2, 2], plain22[:], gates[2], MULT)
        for c in range(HALVES):
            turn_and_add(2, c, accs[c][:], range(D))
            nc.scalar.copy(*z_views(2, c, accs[c][:]))

        accs = [psum.tile([P, P], F32, name=f"z_acc3_{c}", tag=bank) for c, bank in enumerate(("z2", "z3"))]
        terms3 = keep.tile([P, HALVES, D, P], F32, name="u3", align_bytes=GRID)
        for c, turns in enumerate(((2, 1, 0), (0, 1, 2))):
            cols = slice(c * P, (c + 1) * P)
            for d in turns:
                if (c, d) in by_scalar:
                    values = plain[:, by_scalar.index((c, d)), :]
                else:
                    values = h[3][:].indirect(pos_t[d][:, cols.start // LIST_ROWS : cols.stop // LIST_ROWS])
                nc.vector.tensor_tensor(terms3[:, c, d, :], values, gates[d][:, cols], MULT)
            for i, d in enumerate(turns):
                nc.tensor.matmul(accs[c][:], terms3[:, c, d, :], ident[:], start=(i == 0), stop=(i == D - 1), is_transpose=True)

        w2_grouped = keep.tile([P, N, PACK], BF16, name="w2g", tag="h3", align_bytes=GRID)
        nc.vector.tensor_copy(*interleave(w2_grouped[:], w2_raw[:]))

        backs = []
        for c in range(HALVES):
            copy = nc.scalar.copy if c == 0 else nc.vector.tensor_copy
            dst, src = z_views(3, c, accs[c][:])
            if c == 0:
                copy(dst, src)
            else:
                for a in range(2):
                    copy(dst[:, a], src[:, a])
            back = psum.tile([P, 2, P], F32, name=f"back{c}", tag=("hD", "z0")[c])
            pairs = z_turned[c][:].rearrange("v a p e -> v (a p e)").bitcast(F32)
            for a in range(2):
                nc.tensor.transpose(back[:, a, :], pairs[:, a * P : (a + 1) * P], ident[:])
            backs.append(back)
        w2_codes = keep.tile([P, N], U32, name="w2_codes", align_bytes=GRID)
        quantize(w2_codes[:], w2_scales[:], w2_grouped[:].rearrange("p m j -> p (m j)"))
        for c, back in enumerate(backs):
            copy = nc.scalar.copy if c == 0 else nc.vector.tensor_copy
            z_grouped = keep.tile([P, P * PACK], BF16, name=f"zg{c}", align_bytes=GRID)
            z_codes = keep.tile([P, P], U32, name=f"z_codes{c}", align_bytes=GRID)
            z_scales = keep.tile([P, P], U8, name=f"z_scales{c}", align_bytes=GRID)
            res = keep.tile([P, P], F32, name=f"res{c}", align_bytes=GRID)
            banks = (("hA",), ("z1", "hB"))[c]
            step = P // len(banks)
            for i, bank in enumerate(banks):
                cols = slice(i * step, (i + 1) * step)
                values = z_grouped[:, PACK * cols.start : PACK * cols.stop]
                nc.scalar.copy(values.bitcast(F32).rearrange("p (v a) -> p v a", a=2), back[:, :, cols].rearrange("p a v -> p v a"))
                quantize(z_codes[:, cols], z_scales[:, cols], values)
                o_acc = psum.tile([P, step], F32, name=f"o_acc{bank}", tag=bank)
                nc.tensor.matmul_mx(
                    out=o_acc[:],
                    lhsT=w2_codes[:].bitcast(FP8X4),
                    lhsT_scale=w2_scales[:],
                    rhs=z_codes[:, cols].bitcast(FP8X4),
                    rhs_scale=z_scales[:, cols],
                    start=True,
                    stop=True,
                )
                copy(res[:, cols], o_acc[:])
            nc.sync.dma_start(out[:, c * P : (c + 1) * P], res[:])
